import numpy as np
import ml_dtypes


def mxq(x, axis, fmt="e4m3"):
    dtype, down = {"e4m3": (ml_dtypes.float8_e4m3fn, 7), "e5m2": (ml_dtypes.float8_e5m2, 14)}[fmt]
    v = np.moveaxis(np.asarray(x, np.float32).astype(ml_dtypes.bfloat16).astype(np.float64), axis, -1)
    blocks = v.reshape(v.shape[:-1] + (-1, 32))
    amax = np.abs(blocks).max(-1, keepdims=True)
    byte = np.maximum(np.where(amax > 0, np.frexp(amax)[1] - 1 + 127, 0) - down, 1)
    scale = np.exp2(byte - 127.0)
    codes = (blocks / scale).astype(np.float32).astype(dtype).astype(np.float64)
    return np.moveaxis((codes * scale).reshape(v.shape), -1, axis)


WIDE = False


def mx_kscale(k):
    if not WIDE:
        return np.ones(k)
    levels = np.array([10, -10, 5, -5, 0])
    if k % 512:
        return np.exp2(np.random.permutation(np.resize(levels, k // 32))).repeat(32)
    a = np.empty((k // 512, 16))
    for p in range(k // 512):
        a[p, :8] = np.random.permutation(np.resize(levels, 8))
        for g in range(8):
            far = levels[np.abs(levels - a[p, g]) >= 10]
            a[p, g + 8] = far[np.random.randint(len(far))]
    return np.exp2(a.ravel()).repeat(32)


BF16 = ml_dtypes.bfloat16


def bf(x):
    return np.asarray(x, np.float32).astype(BF16)


def f64(x):
    return np.asarray(x).astype(np.float64)


E2M1 = np.array([0.0, 0.5, 1.0, 1.5, 2.0, 3.0, 4.0, 6.0, -0.0, -0.5, -1.0, -1.5, -2.0, -3.0, -4.0, -6.0])


def pack_weight(w, fmt):
    k, n = w.shape
    w = f64(bf(w)).reshape(k // 32, 32, n)
    amax = np.abs(w).max(1)
    if fmt == "e4m3":
        byte = np.frexp(amax)[1] - 1 + 127 - 7
    else:
        mant, ex = np.frexp(amax / 6.0)
        byte = np.where(mant > 0.5, ex, ex - 1) + 127
    byte = np.clip(np.where(amax > 0, byte, 1), 1, 254)
    scaled = (w * np.exp2(127.0 - byte)[:, None, :]).reshape(k, n).astype(np.float32)
    by_word = np.ascontiguousarray(scaled.reshape(k // 512, 128, 4, n).transpose(0, 1, 3, 2))
    if fmt == "e4m3":
        words = by_word.astype(ml_dtypes.float8_e4m3fn).view(np.uint8)
    else:
        c = by_word.astype(ml_dtypes.float4_e2m1fn).view(np.uint8) & 0xF
        words = c[..., 0::2] | (c[..., 1::2] << 4)
    return np.ascontiguousarray(words), np.ascontiguousarray(byte.astype(np.uint8).reshape(k // 512, 16, n))


def unpack_weight(words, scales, fmt):
    g, p, n, _ = words.shape
    if fmt == "e4m3":
        vals = np.ascontiguousarray(words).view(ml_dtypes.float8_e4m3fn).astype(np.float64)
    else:
        nib = np.empty((g, p, n, 4), np.uint8)
        nib[..., 0::2] = words & 0xF
        nib[..., 1::2] = words >> 4
        vals = E2M1[nib]
    vals = vals * np.repeat(np.exp2(scales.astype(np.float64) - 127.0), 8, axis=1)[..., None]
    return vals.transpose(0, 1, 3, 2).reshape(g * 512, n)
def pack4(w):
    words, scales = pack_weight(w, "e2m1")
    return words.reshape(words.shape[0], 128, -1), scales


def unpack4(words, scales):
    return unpack_weight(words.reshape(words.shape[0], 128, -1, 2), scales, "e2m1")


def planes(Y):
    n, m = Y.shape
    b = f64(bf(Y)).reshape(n // 32, 32, m)
    amax = np.abs(b).max(1)
    byte = np.clip(np.where(amax > 0, np.frexp(amax)[1] - 1 + 127 - 7, 1), 1, 254)
    codes = (b * np.exp2(127.0 - byte)[:, None, :]).reshape(n, m).astype(np.float32).astype(ml_dtypes.float8_e4m3fn).view(np.uint8)
    words = codes.reshape(n // 512, 128, 4, m).transpose(0, 1, 3, 2)
    return np.ascontiguousarray(words), np.ascontiguousarray(byte.astype(np.uint8).reshape(n // 512, 16, m))


M, K, F, N = 2048, 512, 1536, 1024

DEPTH_SPREAD = 0.6
OFFSET_SPREAD = 0.5

def setup_inputs():
    rn = np.random.randn
    s = mx_kscale(K)
    t = mx_kscale(F)
    dtau = DEPTH_SPREAD * rn(M, K) * s
    mix = rn(K, F) ** 2 / np.sqrt(3.0 * K) / s[:, None]
    flux = np.exp(0.4 * rn(F)) * t
    resp = rn(F, N) / np.sqrt(F) / t[:, None]
    mix_words, mix_scales = pack4(mix)
    resp_words, resp_scales = pack4(resp)
    return {"dtau": bf(dtau), "mix_words": mix_words, "mix_scales": mix_scales,
            "flux": bf(flux), "resp_words": resp_words, "resp_scales": resp_scales,
            "mu0": bf(np.random.uniform(0.3, 1.0, M)),
            "offset": bf(OFFSET_SPREAD * rn(N)),
            "rate": bf(np.exp(0.8 * rn(N)))}

def reference(dtau, mix_words, mix_scales, flux, resp_words, resp_scales, mu0, offset, rate):
    mix = unpack4(mix_words, mix_scales)
    resp = unpack4(resp_words, resp_scales)
    depth = mxq(f64(dtau), 1, "e4m3") @ mix
    h = np.exp(-depth) * f64(flux)
    conv = mxq(h, 1, "e4m3") @ resp
    y = (f64(mu0)[:, None] * conv + f64(offset)) * f64(rate)
    words, scales = planes(y.T)
    return y, words, scales

@@ -1,0 +1,409 @@
+from contextlib import ExitStack
+
+import concourse.mybir as mybir
+from concourse.masks import make_identity
+
+M, K, F, N = 2048, 512, 1536, 1024
+FLOPS = 2 * M * K * F + 2 * M * F * N
+
+F32 = mybir.dt.float32
+BF16 = mybir.dt.bfloat16
+I32 = mybir.dt.int32
+U32 = mybir.dt.uint32
+U8 = mybir.dt.uint8
+FP8X4 = mybir.dt.float8_e4m3fn_x4
+FP4X4 = mybir.dt.float4_e2m1fn_x4
+ALU = mybir.AluOpType
+ACT = mybir.ActivationFunctionType
+
+P = 128
+CH = 256
+NCH = M // CH
+NT = M // P
+GF = F // 512
+GN = N // 512
+X_LOADS = [(0, 1), (1, 2), (2, 4), (4, 8)]
+X_AT = {0: [2], 1: [3, 4], 2: [5], 3: [6], 4: [7]}
+XQ_AT = {0: [2], 1: [3], 2: [4], 3: [5], 4: [6], 5: [7]}
+RATE_ON_VECTOR = {(15, 0), (15, 1), (14, 1)}
+SWAP = True
+X14V = True
+
+
+def tile_aerosol_albedo_heating_h1_kernel(
+    tc, dtau, mix_words, mix_scales, flux, resp_words, resp_scales, mu0, offset, rate, out_0, out_1, out_2
+):
+    nc = tc.nc
+    with ExitStack() as ctx:
+        keep = ctx.enter_context(tc.tile_pool(name="keep", bufs=1))
+        work = ctx.enter_context(tc.tile_pool(name="work", bufs=1))
+        psum = ctx.enter_context(tc.psum_pool(name="psum", bufs=1))
+        ctx.enter_context(tc.manual_schedule())
+
+        ident = keep.tile([P, P], F32, name="ident")
+        vec_raw = keep.tile([P, 512], BF16, name="vec_raw")
+        vec_rows = keep.tile([P, 4, P], F32, name="vec_rows")
+        warm = keep.tile([P, 8], F32, name="warm")
+        mix_sc_raw = keep.tile([P, F], U8, name="mix_sc_raw", align_bytes=64)
+        mix_w_raw = [keep.tile([P, 1024], U8, name="mix_w_raw0"), keep.tile([P, 2048], U8, name="mix_w_raw1")]
+        mix_w = keep.tile([P, GF, 4, 256], U8, name="mix_w", align_bytes=64)
+        mix_sc = keep.tile([P, GF, 4, P], U8, name="mix_sc", align_bytes=64)
+        resp_w = keep.tile([P, GF, 2 * N], U8, name="resp_w", align_bytes=64)
+        resp_sc = keep.tile([P, GF, N], U8, name="resp_sc", align_bytes=64)
+        offset_bc = keep.tile([P, N], BF16, name="offset_bc")
+        rate_bc = keep.tile([P, N], BF16, name="rate_bc")
+        y_sc = keep.tile([P, GN, M - 2 * CH], U8, name="y_sc", align_bytes=64)
+        y_sc_last = keep.tile([P, GN, 2 * CH], U8, name="y_sc_last", align_bytes=64)
+        consts = psum.tile([P, 4, P], F32, name="consts")
+
+        x_sb = {}
+
+        def load_x(c0, c1):
+            t = keep.tile([P, 2 * (c1 - c0), K], BF16, name="x%d" % c0)
+            nc.sync.dma_start(out=t[:], in_=dtau[CH * c0 : CH * c1, :].rearrange("(j p) k -> p j k", p=P))
+            for c in range(c0, c1):
+                x_sb[c] = t[:, 2 * (c - c0) : 2 * (c - c0) + 2, :]
+
+        nc.vector.memset(mix_sc_raw[:].bitcast(I32), 0)
+        nc.vector.memset(warm[:], 0.0)
+        nc.vector.memset(resp_sc[:].rearrange("p g n -> p (g n)").bitcast(I32), 0)
+        nc.gpsimd.dma_start(out=vec_raw[0:GF, :], in_=flux.rearrange("(g k) -> g k", g=GF))
+        nc.gpsimd.dma_start(out=vec_raw[32 : 32 + NT, 0:P], in_=mu0.rearrange("(i p) -> i p", p=P))
+        nc.scalar.activation(out=warm[:, 4:8], in_=warm[:, 0:4], func=ACT.Exp)
+        make_identity(nc, ident[:])
+        nc.gpsimd.memset(vec_rows[:], 0.0)
+
+        load_x(*X_LOADS[0])
+        nc.sync.dma_start(out=mix_w_raw[0][:].bitcast(I32), in_=mix_words[0, :, 0:1024].bitcast(I32))
+        for q in range(4):
+            nc.sync.dma_start(
+                out=mix_sc_raw[32 * q : 32 * q + 4, :].bitcast(I32), in_=mix_scales[0, 4 * q : 4 * q + 4, :].bitcast(I32)
+            )
+        load_x(*X_LOADS[1])
+        nc.sync.dma_start(out=mix_w_raw[1][:].bitcast(I32), in_=mix_words[0, :, 1024:3072].bitcast(I32))
+        for q in range(4):
+            nc.sync.dma_start(
+                out=resp_sc[32 * q : 32 * q + 4, :, :].bitcast(I32),
+                in_=resp_scales[:, 4 * q : 4 * q + 4, :].rearrange("g r n -> r g n").bitcast(I32),
+            )
+        load_x(*X_LOADS[2])
+        nc.sync.dma_start(out=resp_w[:].bitcast(I32), in_=resp_words.rearrange("g p b -> p g b").bitcast(I32))
+        nc.sync.dma_start(out=offset_bc[:], in_=offset.partition_broadcast(P))
+        nc.sync.dma_start(out=rate_bc[:], in_=rate.partition_broadcast(P))
+        load_x(*X_LOADS[3])
+
+        def permute_mix(g):
+            src = mix_w_raw[0][:] if g == 0 else mix_w_raw[1][:, 1024 * (g - 1) : 1024 * g]
+            nc.vector.tensor_copy(
+                out=mix_w[:, g, :, :].rearrange("p t (m b) -> p t m b", b=2),
+                in_=src.rearrange("p (m t b) -> p t m b", t=4, b=2),
+            )
+            nc.vector.tensor_copy(
+                out=mix_sc[:, g, :, :], in_=mix_sc_raw[:, 512 * g : 512 * (g + 1)].rearrange("p (m t) -> p t m", t=4)
+            )
+
+        def make_consts():
+            nc.scalar.copy(out=vec_rows[0:GF, :, :], in_=vec_raw[0:GF, :].rearrange("r (p t) -> r t p", t=4))
+            nc.scalar.copy(out=vec_rows[32 : 32 + NT, 0, :], in_=vec_raw[32 : 32 + NT, 0:P])
+            for t in range(4):
+                nc.tensor.transpose(consts[:, t, :], vec_rows[:, t, :], ident[:])
+
+        xt_ps, xt_sb, x_codes, x_scales = {}, {}, {}, {}
+        depth_ps, ex, h_bf, h_codes, h_scales = {}, {}, {}, {}, {}
+        conv_ps, tmp, y, y_bf, yt_ps, yt_sb = {}, {}, {}, {}, {}, {}
+
+        def x_turn(c):
+            xt_ps[c] = psum.tile([P, 2, 2, P], F32, name="turn", tag="turn", bufs=2)
+            for j in range(2):
+                words = x_sb[c][:, j, :].bitcast(F32)
+                for u in range(2):
+                    nc.tensor.transpose(xt_ps[c][:, j, u, :], words[:, u:256:2], ident[:])
+
+        def x_exit(c):
+            xt_sb[c] = work.tile([P, CH * 4], BF16, name="xt_sb", tag="xt_sb", bufs=3, align_bytes=64)
+            nc.scalar.copy(
+                out=xt_sb[c][:].bitcast(F32).rearrange("p (j r u) -> p j r u", j=2, u=2),
+                in_=xt_ps[c][:].rearrange("p j u r -> p j r u"),
+            )
+
+        def x_quant(c):
+            x_codes[c] = work.tile([P, CH], U32, name="x_codes", tag="x_codes", bufs=4, align_bytes=64)
+            x_scales[c] = work.tile([P, CH], U8, name="x_scales", tag="x_scales", bufs=4, align_bytes=64)
+            nc.vector.quantize_mx(out=x_codes[c][:].bitcast(FP8X4), scales=x_scales[c][:], in_=xt_sb[c][:])
+
+        def depth(c, g, u):
+            if not 0 <= c < NCH:
+                return
+            depth_ps[c, g, u] = psum.tile([P, 2, CH], F32, name="depth", tag="depth", bufs=3)
+            for e in range(2):
+                nc.tensor.matmul_mx(
+                    out=depth_ps[c, g, u][:, e, :],
+                    lhsT=mix_w[:, g, 2 * u + e, :].bitcast(FP4X4),
+                    lhsT_scale=mix_sc[:, g, 2 * u + e, :],
+                    rhs=x_codes[c][:].bitcast(FP8X4),
+                    rhs_scale=x_scales[c][:],
+                    start=True,
+                    stop=True,
+                )
+
+        def atten(c, g, u):
+            if not 0 <= c < NCH:
+                return
+            if u == 0:
+                ex[c, g] = work.tile([P, 2, CH, 2], F32, name="ex", tag="ex", bufs=4)
+            nc.scalar.activation(
+                out=ex[c, g][:, u, :, :], in_=depth_ps[c, g, u][:].rearrange("p e m -> p m e"), func=ACT.Exp, scale=-1.0
+            )
+
+        def times_flux(c, g):
+            if not 0 <= c < NCH:
+                return
+            if g == 0:
+                h_bf[c] = work.tile([P, GF, CH * 4], BF16, name="h_bf", tag="h_bf", bufs=2, align_bytes=64)
+            flux_g = consts[:, :, g].rearrange("p (u e) -> p u e", u=2).unsqueeze(1).to_broadcast([P, CH, 2, 2])
+            nc.vector.tensor_tensor(
+                out=h_bf[c][:, g, :].rearrange("p (m u e) -> p m u e", u=2, e=2),
+                in0=ex[c, g][:].rearrange("p u m e -> p m u e"),
+                in1=flux_g,
+                op=ALU.mult,
+            )
+
+        def h_quant(c, g0, g1):
+            if not 0 <= c < NCH:
+                return
+            if g0 == 0:
+                h_codes[c] = work.tile([P, GF * CH], U32, name="h_codes", tag="h_codes", bufs=2, align_bytes=64)
+                h_scales[c] = work.tile([P, GF * CH], U8, name="h_scales", tag="h_scales", bufs=2, align_bytes=64)
+            nc.vector.quantize_mx(
+                out=h_codes[c][:, CH * g0 : CH * g1].bitcast(FP8X4),
+                scales=h_scales[c][:, CH * g0 : CH * g1],
+                in_=h_bf[c][:, g0:g1, :].rearrange("p g x -> p (g x)"),
+            )
+
+        def conv(i, s, tag="conv", bufs=2):
+            if not 0 <= i < NT:
+                return
+            c, j = divmod(i, 2)
+            conv_ps[i, s] = psum.tile([P, 512], F32, name="conv", tag=tag, bufs=bufs)
+            for g in range(GF):
+                cols = slice(CH * g + P * j, CH * g + P * (j + 1))
+                nc.tensor.matmul_mx(
+                    out=conv_ps[i, s][:],
+                    lhsT=h_codes[c][:, cols].bitcast(FP8X4),
+                    lhsT_scale=h_scales[c][:, cols],
+                    rhs=resp_w[:, g, 1024 * s : 1024 * (s + 1)].bitcast(FP4X4),
+                    rhs_scale=resp_sc[:, g, 512 * s : 512 * (s + 1)],
+                    start=(g == 0),
+                    stop=(g == GF - 1),
+                )
+
+        def sunlit(i, s):
+            if not 0 <= i < NT:
+                return
+            tmp[i, s] = work.tile([P, 512], F32, name="tmp", tag="tmp", bufs=6)
+            nc.vector.scalar_tensor_tensor(
+                out=tmp[i, s][:],
+                in0=conv_ps[i, s][:],
+                scalar=consts[:, 0, 32 + i : 33 + i],
+                in1=offset_bc[:, 512 * s : 512 * (s + 1)],
+                op0=ALU.mult,
+                op1=ALU.add,
+            )
+
+        def times_rate(i, s):
+            if not 0 <= i < NT:
+                return
+            if s == 0:
+                y[i] = work.tile([P, N], F32, name="y", tag="y", bufs=4)
+            eng = nc.vector if (i, s) in RATE_ON_VECTOR else nc.gpsimd
+            cols = slice(512 * s, 512 * (s + 1))
+            eng.tensor_tensor(out=y[i][:, cols], in0=tmp[i, s][:], in1=rate_bc[:, cols], op=ALU.mult)
+
+        def store_y(i, s0=0, s1=GN):
+            if not 0 <= i < NT:
+                return
+            cols = slice(512 * s0, 512 * s1)
+            nc.sync.dma_start(out=out_0[P * i : P * (i + 1), cols], in_=y[i][:, cols])
+
+        def y_round(i, s):
+            if not 0 <= i < NT:
+                return
+            if s == 0:
+                y_bf[i] = work.tile([P, GN, 2, P, 2], BF16, name="y_bf", tag="y_bf", bufs=3)
+            nc.scalar.copy(
+                out=y_bf[i][:, s, :, :, :],
+                in_=y[i][:, 512 * s : 512 * (s + 1)].rearrange("p (q u e) -> p u q e", u=2, e=2),
+            )
+
+        def y_round_direct(i, s):
+            cols = slice(512 * s, 512 * (s + 1))
+            nc.vector.tensor_tensor(
+                out=y_bf[i][:, s, :, :, :],
+                in0=tmp[i, s][:].rearrange("p (q u e) -> p u q e", u=2, e=2),
+                in1=rate_bc[:, cols].rearrange("p (q u e) -> p u q e", u=2, e=2),
+                op=ALU.mult,
+            )
+
+        def y_turn(i, s0=0, s1=GN, tag="turn", bufs=2):
+            if not 0 <= i < NT:
+                return
+            yt_ps[i, s0] = psum.tile([P, s1 - s0, 2, P], F32, name="turn", tag=tag, bufs=bufs)
+            for s in range(s0, s1):
+                for u in range(2):
+                    words = y_bf[i][:, s, u, :, :].rearrange("p q e -> p (q e)").bitcast(F32)
+                    nc.tensor.transpose(yt_ps[i, s0][:, s - s0, u, :], words, ident[:])
+
+        def y_exit(i, s0=0, s1=GN, on_vector=False):
+            if not 0 <= i < NT:
+                return
+            c, j = divmod(i, 2)
+            if j == 0 and s0 == 0:
+                yt_sb[c] = work.tile([P, GN, CH * 4], BF16, name="yt_sb", tag="yt_sb", bufs=3, align_bytes=64)
+            (nc.vector.tensor_copy if on_vector else nc.scalar.copy)(
+                out=yt_sb[c][:, s0:s1, 512 * j : 512 * (j + 1)].bitcast(F32).rearrange("p s (r u) -> p s r u", u=2),
+                in_=yt_ps[i, s0][:].rearrange("p s u r -> p s r u"),
+            )
+
+        y_codes = {}
+
+        def y_quant(c, s0=0, s1=GN, j0=0, j1=2):
+            if not 0 <= c < NCH:
+                return
+            if c not in y_codes:
+                y_codes[c] = work.tile([P, GN, CH], U32, name="y_codes", tag="y_codes", bufs=3, align_bytes=64)
+            plane, m0 = (y_sc, CH * c) if c < NCH - 2 else (y_sc_last, CH * (c - NCH + 2))
+            for s in range(s0, s1):
+                nc.vector.quantize_mx(
+                    out=y_codes[c][:, s, P * j0 : P * j1].bitcast(FP8X4),
+                    scales=plane[:, s, m0 + P * j0 : m0 + P * j1],
+                    in_=yt_sb[c][:, s, 512 * j0 : 512 * j1],
+                )
+
+        def store_codes(c, s0=0, s1=GN, j0=0, j1=2):
+            if not 0 <= c < NCH:
+                return
+            nc.sync.dma_start(
+                out=out_1[s0:s1, :, CH * c + P * j0 : CH * c + P * j1, :].rearrange("g p m t -> p g (m t)").bitcast(I32),
+                in_=y_codes[c][:, s0:s1, P * j0 : P * j1].bitcast(I32),
+            )
+
+        def store_scales(m0, m1, src, engs):
+            for q in range(4):
+                engs[q].dma_start(
+                    out=out_2[:, 4 * q : 4 * q + 4, m0:m1].rearrange("g r m -> r g m").bitcast(I32),
+                    in_=src[32 * q : 32 * q + 4, :, :].bitcast(I32),
+                )
+
+        x_turn(0)
+        x_exit(0)
+        x_turn(1)
+        permute_mix(0)
+        x_quant(0)
+        x_exit(1)
+        depth(0, 0, 0)
+        depth(0, 0, 1)
+        make_consts()
+        permute_mix(1)
+        depth(0, 1, 0)
+        atten(0, 0, 0)
+        atten(0, 0, 1)
+        depth(0, 1, 1)
+        permute_mix(2)
+        x_quant(1)
+        for k in range(NCH):
+            a, b = 2 * k - 3, 2 * k - 2
+            for s in range(2):
+                sunlit(a, s)
+            for s in range(2):
+                times_rate(a, s)
+            store_y(a)
+            depth(k, 2, 0)
+            conv(b, 0)
+            y_round(a - 1, 1)
+            atten(k, 1, 0)
+            if SWAP:
+                conv(b, 1)
+            depth(k, 2, 1)
+            if not SWAP:
+                conv(b, 1)
+            atten(k, 1, 1)
+            atten(k, 2, 0)
+            y_round(a, 0)
+            atten(k, 2, 1)
+            times_flux(k, 0)
+            for s in range(2):
+                sunlit(b, s)
+            for s in range(2):
+                times_rate(b, s)
+            store_y(b)
+            y_turn(a - 1)
+            for c in X_AT.get(k, []):
+                x_turn(c)
+            depth(k + 1, 0, 0)
+            conv(b + 1, 0)
+            y_exit(a - 1)
+            y_round(a, 1)
+            for c in X_AT.get(k, []):
+                x_exit(c)
+            atten(k + 1, 0, 0)
+            y_turn(a)
+            depth(k + 1, 0, 1)
+            conv(b + 1, 1)
+            depth(k + 1, 1, 0)
+            y_exit(a)
+            y_round(b, 0)
+            atten(k + 1, 0, 1)
+            depth(k + 1, 1, 1)
+            times_flux(k, 1)
+            times_flux(k, 2)
+            h_quant(k, 0, 2)
+            for c in XQ_AT.get(k, []):
+                x_quant(c)
+            h_quant(k, 2, 3)
+            y_quant(k - 2)
+            store_codes(k - 2)
+        store_scales(0, M - 2 * CH, y_sc, [nc.sync] * 4)
+        conv(14, 0, "depth", 3)
+        y_round(12, 1)
+        y_turn(12)
+        conv(14, 1, "depth", 3)
+        conv(15, 0, "depth", 3)
+        sunlit(13, 0)
+        sunlit(13, 1)
+        conv(15, 1)
+        times_rate(13, 0)
+        times_rate(13, 1)
+        store_y(13)
+        sunlit(14, 0)
+        sunlit(14, 1)
+        y_exit(12)
+        y_round(13, 0)
+        y_round(13, 1)
+        y_turn(13)
+        sunlit(15, 0)
+        sunlit(15, 1)
+        times_rate(14, 0)
+        times_rate(14, 1)
+        store_y(14)
+        times_rate(15, 0)
+        store_y(15, 0, 1)
+        y_exit(13)
+        y_round(14, 0)
+        y_round(14, 1)
+        y_turn(14)
+        y_round(15, 0)
+        y_round_direct(15, 1)
+        times_rate(15, 1)
+        store_y(15, 1, 2)
+        y_turn(15, 1, 2, "depth", 3)
+        y_turn(15, 0, 1, "depth", 3)
+        y_quant(6)
+        store_codes(6)
+        y_exit(14)
+        y_exit(15, 1, 2, on_vector=True)
+        y_exit(15, 0, 1)
+        y_quant(7, 0, 2, 0, 1)
+        y_quant(7, 1, 2, 1, 2)
+        y_quant(7, 0, 1, 1, 2)
+        store_codes(7)
+        store_scales(M - 2 * CH, M, y_sc_last, [nc.scalar, nc.sync, nc.scalar, nc.sync])

@@ -23,11 +23,8 @@ NT = M // P
 GF = F // 512
 GN = N // 512
 X_LOADS = [(0, 1), (1, 2), (2, 4), (4, 8)]
-X_AT = {0: [2], 1: [3, 4], 2: [5], 3: [6], 4: [7]}
-XQ_AT = {0: [2], 1: [3], 2: [4], 3: [5], 4: [6], 5: [7]}
-RATE_ON_VECTOR = {(15, 0), (15, 1), (14, 1)}
-SWAP = True
-X14V = True
+X_AT = {0: [2, 3], 1: [4, 5], 4: [6], 5: [7]}
+LATE = 3
 
 
 def tile_aerosol_albedo_heating_h1_kernel(
@@ -52,8 +49,8 @@ def tile_aerosol_albedo_heating_h1_kernel(
         resp_sc = keep.tile([P, GF, N], U8, name="resp_sc", align_bytes=64)
         offset_bc = keep.tile([P, N], BF16, name="offset_bc")
         rate_bc = keep.tile([P, N], BF16, name="rate_bc")
-        y_sc = keep.tile([P, GN, M - 2 * CH], U8, name="y_sc", align_bytes=64)
-        y_sc_last = keep.tile([P, GN, 2 * CH], U8, name="y_sc_last", align_bytes=64)
+        y_sc = keep.tile([P, NCH - LATE, GN, CH], U8, name="y_sc", align_bytes=64)
+        y_sc_last = keep.tile([P, GN, LATE * CH], U8, name="y_sc_last", align_bytes=64)
         consts = psum.tile([P, 4, P], F32, name="consts")
 
         x_sb = {}
@@ -102,14 +99,16 @@ def tile_aerosol_albedo_heating_h1_kernel(
                 out=mix_sc[:, g, :, :], in_=mix_sc_raw[:, 512 * g : 512 * (g + 1)].rearrange("p (m t) -> p t m", t=4)
             )
 
-        def make_consts():
+        def cast_vectors():
             nc.scalar.copy(out=vec_rows[0:GF, :, :], in_=vec_raw[0:GF, :].rearrange("r (p t) -> r t p", t=4))
             nc.scalar.copy(out=vec_rows[32 : 32 + NT, 0, :], in_=vec_raw[32 : 32 + NT, 0:P])
+
+        def turn_vectors():
             for t in range(4):
                 nc.tensor.transpose(consts[:, t, :], vec_rows[:, t, :], ident[:])
 
-        xt_ps, xt_sb, x_codes, x_scales = {}, {}, {}, {}
-        depth_ps, ex, h_bf, h_codes, h_scales = {}, {}, {}, {}, {}
+        xt_ps = {}
+        depth_ps, ex, h_bf, codes, scales = {}, {}, {}, {}, {}
         conv_ps, tmp, y, y_bf, yt_ps, yt_sb = {}, {}, {}, {}, {}, {}
 
         def x_turn(c):
@@ -119,17 +118,26 @@ def tile_aerosol_albedo_heating_h1_kernel(
                 for u in range(2):
                     nc.tensor.transpose(xt_ps[c][:, j, u, :], words[:, u:256:2], ident[:])
 
-        def x_exit(c):
-            xt_sb[c] = work.tile([P, CH * 4], BF16, name="xt_sb", tag="xt_sb", bufs=3, align_bytes=64)
-            nc.scalar.copy(
-                out=xt_sb[c][:].bitcast(F32).rearrange("p (j r u) -> p j r u", j=2, u=2),
+        def operand_tiles(c):
+            if c not in h_bf:
+                h_bf[c] = work.tile([P, GF + 1, CH * 4], BF16, name="h_bf", tag="h_bf", bufs=5, align_bytes=64)
+            return h_bf[c]
+
+        def x_exit(c, on_vector=False):
+            (nc.vector.tensor_copy if on_vector else nc.scalar.copy)(
+                out=operand_tiles(c - 2)[:, GF, :].bitcast(F32).rearrange("p (j r u) -> p j r u", j=2, u=2),
                 in_=xt_ps[c][:].rearrange("p j u r -> p j r u"),
             )
 
-        def x_quant(c):
-            x_codes[c] = work.tile([P, CH], U32, name="x_codes", tag="x_codes", bufs=4, align_bytes=64)
-            x_scales[c] = work.tile([P, CH], U8, name="x_scales", tag="x_scales", bufs=4, align_bytes=64)
-            nc.vector.quantize_mx(out=x_codes[c][:].bitcast(FP8X4), scales=x_scales[c][:], in_=xt_sb[c][:])
+        def quant(c, g0, g1):
+            if c not in codes:
+                codes[c] = work.tile([P, (GF + 1) * CH], U32, name="codes", tag="codes", bufs=4, align_bytes=64)
+                scales[c] = work.tile([P, (GF + 1) * CH], U8, name="scales", tag="scales", bufs=4, align_bytes=64)
+            nc.vector.quantize_mx(
+                out=codes[c][:, CH * g0 : CH * g1].bitcast(FP8X4),
+                scales=scales[c][:, CH * g0 : CH * g1],
+                in_=h_bf[c][:, g0:g1, :].rearrange("p g x -> p (g x)"),
+            )
 
         def depth(c, g, u):
             if not 0 <= c < NCH:
@@ -140,8 +148,8 @@ def tile_aerosol_albedo_heating_h1_kernel(
                     out=depth_ps[c, g, u][:, e, :],
                     lhsT=mix_w[:, g, 2 * u + e, :].bitcast(FP4X4),
                     lhsT_scale=mix_sc[:, g, 2 * u + e, :],
-                    rhs=x_codes[c][:].bitcast(FP8X4),
-                    rhs_scale=x_scales[c][:],
+                    rhs=codes[c - 2][:, GF * CH :].bitcast(FP8X4),
+                    rhs_scale=scales[c - 2][:, GF * CH :],
                     start=True,
                     stop=True,
                 )
@@ -149,35 +157,19 @@ def tile_aerosol_albedo_heating_h1_kernel(
         def atten(c, g, u):
             if not 0 <= c < NCH:
                 return
-            if u == 0:
-                ex[c, g] = work.tile([P, 2, CH, 2], F32, name="ex", tag="ex", bufs=4)
+            if c not in ex:
+                ex[c] = work.tile([P, 2, GF, CH, 2], F32, name="ex", tag="ex", bufs=2)
             nc.scalar.activation(
-                out=ex[c, g][:, u, :, :], in_=depth_ps[c, g, u][:].rearrange("p e m -> p m e"), func=ACT.Exp, scale=-1.0
+                out=ex[c][:, u, g, :, :], in_=depth_ps[c, g, u][:].rearrange("p e m -> p m e"), func=ACT.Exp, scale=-1.0
             )
 
-        def times_flux(c, g):
-            if not 0 <= c < NCH:
-                return
-            if g == 0:
-                h_bf[c] = work.tile([P, GF, CH * 4], BF16, name="h_bf", tag="h_bf", bufs=2, align_bytes=64)
-            flux_g = consts[:, :, g].rearrange("p (u e) -> p u e", u=2).unsqueeze(1).to_broadcast([P, CH, 2, 2])
+        def times_flux(c, g0, g1):
+            shape = [P, g1 - g0, CH, 2, 2]
             nc.vector.tensor_tensor(
-                out=h_bf[c][:, g, :].rearrange("p (m u e) -> p m u e", u=2, e=2),
-                in0=ex[c, g][:].rearrange("p u m e -> p m u e"),
-                in1=flux_g,
+                out=operand_tiles(c)[:, g0:g1, :].rearrange("p g (m u e) -> p g m u e", u=2, e=2),
+                in0=ex[c][:, :, g0:g1, :, :].rearrange("p u g m e -> p g m u e"),
+                in1=consts[:, :, g0:g1].rearrange("p (u e) g -> p g u e", u=2).unsqueeze(2).to_broadcast(shape),
                 op=ALU.mult,
-            )
-
-        def h_quant(c, g0, g1):
-            if not 0 <= c < NCH:
-                return
-            if g0 == 0:
-                h_codes[c] = work.tile([P, GF * CH], U32, name="h_codes", tag="h_codes", bufs=2, align_bytes=64)
-                h_scales[c] = work.tile([P, GF * CH], U8, name="h_scales", tag="h_scales", bufs=2, align_bytes=64)
-            nc.vector.quantize_mx(
-                out=h_codes[c][:, CH * g0 : CH * g1].bitcast(FP8X4),
-                scales=h_scales[c][:, CH * g0 : CH * g1],
-                in_=h_bf[c][:, g0:g1, :].rearrange("p g x -> p (g x)"),
             )
 
         def conv(i, s, tag="conv", bufs=2):
@@ -189,8 +181,8 @@ def tile_aerosol_albedo_heating_h1_kernel(
                 cols = slice(CH * g + P * j, CH * g + P * (j + 1))
                 nc.tensor.matmul_mx(
                     out=conv_ps[i, s][:],
-                    lhsT=h_codes[c][:, cols].bitcast(FP8X4),
-                    lhsT_scale=h_scales[c][:, cols],
+                    lhsT=codes[c][:, cols].bitcast(FP8X4),
+                    lhsT_scale=scales[c][:, cols],
                     rhs=resp_w[:, g, 1024 * s : 1024 * (s + 1)].bitcast(FP4X4),
                     rhs_scale=resp_sc[:, g, 512 * s : 512 * (s + 1)],
                     start=(g == 0),
@@ -200,24 +192,25 @@ def tile_aerosol_albedo_heating_h1_kernel(
         def sunlit(i, s):
             if not 0 <= i < NT:
                 return
-            tmp[i, s] = work.tile([P, 512], F32, name="tmp", tag="tmp", bufs=6)
+            if i not in tmp:
+                tmp[i] = work.tile([P, N], F32, name="tmp", tag="tmp", bufs=3)
+            cols = slice(512 * s, 512 * (s + 1))
             nc.vector.scalar_tensor_tensor(
-                out=tmp[i, s][:],
+                out=tmp[i][:, cols],
                 in0=conv_ps[i, s][:],
                 scalar=consts[:, 0, 32 + i : 33 + i],
-                in1=offset_bc[:, 512 * s : 512 * (s + 1)],
+                in1=offset_bc[:, cols],
                 op0=ALU.mult,
                 op1=ALU.add,
             )
 
-        def times_rate(i, s):
+        def times_rate(i, s0=0, s1=GN, eng=nc.gpsimd):
             if not 0 <= i < NT:
                 return
-            if s == 0:
+            if i not in y:
                 y[i] = work.tile([P, N], F32, name="y", tag="y", bufs=4)
-            eng = nc.vector if (i, s) in RATE_ON_VECTOR else nc.gpsimd
-            cols = slice(512 * s, 512 * (s + 1))
-            eng.tensor_tensor(out=y[i][:, cols], in0=tmp[i, s][:], in1=rate_bc[:, cols], op=ALU.mult)
+            cols = slice(512 * s0, 512 * s1)
+            eng.tensor_tensor(out=y[i][:, cols], in0=tmp[i][:, cols], in1=rate_bc[:, cols], op=ALU.mult)
 
         def store_y(i, s0=0, s1=GN):
             if not 0 <= i < NT:
@@ -225,21 +218,23 @@ def tile_aerosol_albedo_heating_h1_kernel(
             cols = slice(512 * s0, 512 * s1)
             nc.sync.dma_start(out=out_0[P * i : P * (i + 1), cols], in_=y[i][:, cols])
 
-        def y_round(i, s):
+        def y_round(i, s0=0, s1=GN):
             if not 0 <= i < NT:
                 return
-            if s == 0:
-                y_bf[i] = work.tile([P, GN, 2, P, 2], BF16, name="y_bf", tag="y_bf", bufs=3)
+            if i not in y_bf:
+                y_bf[i] = work.tile([P, 2, GN, P, 2], BF16, name="y_bf", tag="y_bf", bufs=4)
             nc.scalar.copy(
-                out=y_bf[i][:, s, :, :, :],
-                in_=y[i][:, 512 * s : 512 * (s + 1)].rearrange("p (q u e) -> p u q e", u=2, e=2),
+                out=y_bf[i][:, :, s0:s1, :, :],
+                in_=y[i][:, 512 * s0 : 512 * s1].rearrange("p (s q u e) -> p u s q e", q=P, u=2, e=2),
             )
 
         def y_round_direct(i, s):
+            if i not in y_bf:
+                y_bf[i] = work.tile([P, 2, GN, P, 2], BF16, name="y_bf", tag="y_bf", bufs=4)
             cols = slice(512 * s, 512 * (s + 1))
             nc.vector.tensor_tensor(
-                out=y_bf[i][:, s, :, :, :],
-                in0=tmp[i, s][:].rearrange("p (q u e) -> p u q e", u=2, e=2),
+                out=y_bf[i][:, :, s, :, :],
+                in0=tmp[i][:, cols].rearrange("p (q u e) -> p u q e", u=2, e=2),
                 in1=rate_bc[:, cols].rearrange("p (q u e) -> p u q e", u=2, e=2),
                 op=ALU.mult,
             )
@@ -250,14 +245,14 @@ def tile_aerosol_albedo_heating_h1_kernel(
             yt_ps[i, s0] = psum.tile([P, s1 - s0, 2, P], F32, name="turn", tag=tag, bufs=bufs)
             for s in range(s0, s1):
                 for u in range(2):
-                    words = y_bf[i][:, s, u, :, :].rearrange("p q e -> p (q e)").bitcast(F32)
+                    words = y_bf[i][:, u, s, :, :].rearrange("p q e -> p (q e)").bitcast(F32)
                     nc.tensor.transpose(yt_ps[i, s0][:, s - s0, u, :], words, ident[:])
 
         def y_exit(i, s0=0, s1=GN, on_vector=False):
             if not 0 <= i < NT:
                 return
             c, j = divmod(i, 2)
-            if j == 0 and s0 == 0:
+            if c not in yt_sb:
                 yt_sb[c] = work.tile([P, GN, CH * 4], BF16, name="yt_sb", tag="yt_sb", bufs=3, align_bytes=64)
             (nc.vector.tensor_copy if on_vector else nc.scalar.copy)(
                 out=yt_sb[c][:, s0:s1, 512 * j : 512 * (j + 1)].bitcast(F32).rearrange("p s (r u) -> p s r u", u=2),
@@ -271,11 +266,18 @@ def tile_aerosol_albedo_heating_h1_kernel(
                 return
             if c not in y_codes:
                 y_codes[c] = work.tile([P, GN, CH], U32, name="y_codes", tag="y_codes", bufs=3, align_bytes=64)
-            plane, m0 = (y_sc, CH * c) if c < NCH - 2 else (y_sc_last, CH * (c - NCH + 2))
+            if c < NCH - LATE:
+                nc.vector.quantize_mx(
+                    out=y_codes[c][:].rearrange("p s m -> p (s m)").bitcast(FP8X4),
+                    scales=y_sc[:, c, :, :].rearrange("p s m -> p (s m)"),
+                    in_=yt_sb[c][:].rearrange("p s x -> p (s x)"),
+                )
+                return
+            m0 = CH * (c - NCH + LATE)
             for s in range(s0, s1):
                 nc.vector.quantize_mx(
                     out=y_codes[c][:, s, P * j0 : P * j1].bitcast(FP8X4),
-                    scales=plane[:, s, m0 + P * j0 : m0 + P * j1],
+                    scales=y_sc_last[:, s, m0 + P * j0 : m0 + P * j1],
                     in_=yt_sb[c][:, s, 512 * j0 : 512 * j1],
                 )
 
@@ -294,116 +296,129 @@ def tile_aerosol_albedo_heating_h1_kernel(
                     in_=src[32 * q : 32 * q + 4, :, :].bitcast(I32),
                 )
 
+        def store_early_scales():
+            for s in range(GN):
+                for q in range(4):
+                    nc.sync.dma_start(
+                        out=out_2[s, 4 * q : 4 * q + 4, 0 : M - LATE * CH].rearrange("r (c m) -> r c m", m=CH).bitcast(I32),
+                        in_=y_sc[32 * q : 32 * q + 4, :, s, :].bitcast(I32),
+                    )
+
         x_turn(0)
         x_exit(0)
         x_turn(1)
         permute_mix(0)
-        x_quant(0)
+        quant(-2, GF, GF + 1)
+        cast_vectors()
         x_exit(1)
         depth(0, 0, 0)
         depth(0, 0, 1)
-        make_consts()
         permute_mix(1)
         depth(0, 1, 0)
+        turn_vectors()
         atten(0, 0, 0)
         atten(0, 0, 1)
         depth(0, 1, 1)
+        atten(0, 1, 0)
         permute_mix(2)
-        x_quant(1)
+        depth(0, 2, 0)
+        quant(-1, GF, GF + 1)
         for k in range(NCH):
             a, b = 2 * k - 3, 2 * k - 2
-            for s in range(2):
-                sunlit(a, s)
-            for s in range(2):
-                times_rate(a, s)
+            sunlit(a, 1)
+            y_quant(k - 3)
+            store_codes(k - 3)
+            times_rate(a)
             store_y(a)
-            depth(k, 2, 0)
             conv(b, 0)
-            y_round(a - 1, 1)
-            atten(k, 1, 0)
-            if SWAP:
-                conv(b, 1)
             depth(k, 2, 1)
-            if not SWAP:
-                conv(b, 1)
+            conv(b, 1)
             atten(k, 1, 1)
+            y_round(a - 1)
             atten(k, 2, 0)
-            y_round(a, 0)
             atten(k, 2, 1)
-            times_flux(k, 0)
-            for s in range(2):
-                sunlit(b, s)
-            for s in range(2):
-                times_rate(b, s)
+            depth(k + 1, 0, 0)
+            times_flux(k, 0, 1)
+            sunlit(b, 0)
+            sunlit(b, 1)
+            times_rate(b)
+            if k == NCH - 1:
+                store_early_scales()
             store_y(b)
             y_turn(a - 1)
             for c in X_AT.get(k, []):
                 x_turn(c)
-            depth(k + 1, 0, 0)
-            conv(b + 1, 0)
+            atten(k + 1, 0, 0)
             y_exit(a - 1)
-            y_round(a, 1)
+            y_round(a)
             for c in X_AT.get(k, []):
                 x_exit(c)
-            atten(k + 1, 0, 0)
-            y_turn(a)
+            conv(b + 1, 0)
             depth(k + 1, 0, 1)
             conv(b + 1, 1)
+            atten(k + 1, 0, 1)
+            y_turn(a)
             depth(k + 1, 1, 0)
             y_exit(a)
-            y_round(b, 0)
-            atten(k + 1, 0, 1)
+            atten(k + 1, 1, 0)
             depth(k + 1, 1, 1)
-            times_flux(k, 1)
-            times_flux(k, 2)
-            h_quant(k, 0, 2)
-            for c in XQ_AT.get(k, []):
-                x_quant(c)
-            h_quant(k, 2, 3)
-            y_quant(k - 2)
-            store_codes(k - 2)
-        store_scales(0, M - 2 * CH, y_sc, [nc.sync] * 4)
-        conv(14, 0, "depth", 3)
-        y_round(12, 1)
-        y_turn(12)
-        conv(14, 1, "depth", 3)
-        conv(15, 0, "depth", 3)
-        sunlit(13, 0)
+            depth(k + 1, 2, 0)
+            if k == 0:
+                times_flux(k, 1, 2)
+                times_flux(k, 2, 3)
+            else:
+                times_flux(k, 1, 3)
+            sunlit(b + 1, 0)
+            if k < NCH - 2:
+                quant(k, 0, GF + 1)
+            else:
+                quant(k, 0, 2)
+                quant(k, 2, 3)
+        y_quant(5)
+        store_codes(5)
         sunlit(13, 1)
+        times_rate(13, 1, 2)
+        store_y(13, 1, 2)
+        times_rate(13, 0, 1)
+        store_y(13, 0, 1)
+        y_round(12)
+        conv(14, 0, "depth", 3)
+        conv(14, 1, "depth", 3)
+        y_turn(12)
+        conv(15, 0, "depth", 3)
         conv(15, 1)
-        times_rate(13, 0)
-        times_rate(13, 1)
-        store_y(13)
         sunlit(14, 0)
         sunlit(14, 1)
-        y_exit(12)
-        y_round(13, 0)
-        y_round(13, 1)
-        y_turn(13)
         sunlit(15, 0)
         sunlit(15, 1)
-        times_rate(14, 0)
-        times_rate(14, 1)
-        store_y(14)
-        times_rate(15, 0)
-        store_y(15, 0, 1)
+        y_exit(12)
+        y_round(13, 1, 2)
+        y_round(13, 0, 1)
+        y_turn(13)
+        times_rate(14, 0, 1)
+        store_y(14, 0, 1)
+        times_rate(14, 1, 2, nc.vector)
+        store_y(14, 1, 2)
         y_exit(13)
-        y_round(14, 0)
-        y_round(14, 1)
-        y_turn(14)
-        y_round(15, 0)
+        y_round(14, 0, 1)
+        y_round(14, 1, 2)
+        times_rate(15, 0, 1, nc.vector)
+        store_y(15, 0, 1)
         y_round_direct(15, 1)
-        times_rate(15, 1)
+        times_rate(15, 1, 2, nc.vector)
         store_y(15, 1, 2)
-        y_turn(15, 1, 2, "depth", 3)
-        y_turn(15, 0, 1, "depth", 3)
+        y_round(15, 0, 1)
         y_quant(6)
         store_codes(6)
-        y_exit(14)
+        y_turn(15, 1, 2, "depth", 3)
+        y_turn(14)
+        y_turn(15, 0, 1, "depth", 3)
         y_exit(15, 1, 2, on_vector=True)
-        y_exit(15, 0, 1)
-        y_quant(7, 0, 2, 0, 1)
+        y_exit(14)
+        y_exit(15, 0, 1, on_vector=True)
         y_quant(7, 1, 2, 1, 2)
+        y_quant(7, 0, 2, 0, 1)
+        store_codes(7, 0, 2, 0, 1)
         y_quant(7, 0, 1, 1, 2)
-        store_codes(7)
-        store_scales(M - 2 * CH, M, y_sc_last, [nc.scalar, nc.sync, nc.scalar, nc.sync])
+        store_codes(7, 0, 2, 1, 2)
+        store_scales(M - LATE * CH, M, y_sc_last, [nc.scalar, nc.sync, nc.scalar, nc.sync])

@@ -23,7 +23,7 @@ NT = M // P
 GF = F // 512
 GN = N // 512
 X_LOADS = [(0, 1), (1, 2), (2, 4), (4, 8)]
-X_AT = {0: [2, 3], 1: [4, 5], 4: [6], 5: [7]}
+X_AT = {0: [2], 1: [3, 4], 2: [5], 4: [6], 5: [7]}
 LATE = 3
 
 
@@ -39,6 +39,9 @@ def tile_aerosol_albedo_heating_h1_kernel(
 
         ident = keep.tile([P, P], F32, name="ident")
         vec_raw = keep.tile([P, 512], BF16, name="vec_raw")
+        mu_raw = keep.tile([P, P], BF16, name="mu_raw")
+        rows2 = keep.tile([P, P], F32, name="rows2")
+        cols2 = keep.tile([P, 68], F32, name="cols2")
         vec_rows = keep.tile([P, 4, P], F32, name="vec_rows")
         warm = keep.tile([P, 8], F32, name="warm")
         mix_sc_raw = keep.tile([P, F], U8, name="mix_sc_raw", align_bytes=64)
@@ -65,10 +68,10 @@ def tile_aerosol_albedo_heating_h1_kernel(
         nc.vector.memset(warm[:], 0.0)
         nc.vector.memset(resp_sc[:].rearrange("p g n -> p (g n)").bitcast(I32), 0)
         nc.gpsimd.dma_start(out=vec_raw[0:GF, :], in_=flux.rearrange("(g k) -> g k", g=GF))
-        nc.gpsimd.dma_start(out=vec_raw[32 : 32 + NT, 0:P], in_=mu0.rearrange("(i p) -> i p", p=P))
         nc.scalar.activation(out=warm[:, 4:8], in_=warm[:, 0:4], func=ACT.Exp)
         make_identity(nc, ident[:])
         nc.gpsimd.memset(vec_rows[:], 0.0)
+        nc.gpsimd.memset(rows2[:], 0.0)
 
         load_x(*X_LOADS[0])
         nc.sync.dma_start(out=mix_w_raw[0][:].bitcast(I32), in_=mix_words[0, :, 0:1024].bitcast(I32))
@@ -78,15 +81,16 @@ def tile_aerosol_albedo_heating_h1_kernel(
             )
         load_x(*X_LOADS[1])
         nc.sync.dma_start(out=mix_w_raw[1][:].bitcast(I32), in_=mix_words[0, :, 1024:3072].bitcast(I32))
+        load_x(*X_LOADS[2])
+        nc.sync.dma_start(out=mu_raw[0:NT, :], in_=mu0.rearrange("(i p) -> i p", p=P))
+        nc.sync.dma_start(out=rows2[32:36, :].bitcast(I32), in_=offset.rearrange("(j w) -> j w", j=4).bitcast(I32))
+        nc.sync.dma_start(out=rows2[64:68, :].bitcast(I32), in_=rate.rearrange("(j w) -> j w", j=4).bitcast(I32))
+        nc.sync.dma_start(out=resp_w[:].bitcast(I32), in_=resp_words.rearrange("g p b -> p g b").bitcast(I32))
         for q in range(4):
             nc.sync.dma_start(
                 out=resp_sc[32 * q : 32 * q + 4, :, :].bitcast(I32),
                 in_=resp_scales[:, 4 * q : 4 * q + 4, :].rearrange("g r n -> r g n").bitcast(I32),
             )
-        load_x(*X_LOADS[2])
-        nc.sync.dma_start(out=resp_w[:].bitcast(I32), in_=resp_words.rearrange("g p b -> p g b").bitcast(I32))
-        nc.sync.dma_start(out=offset_bc[:], in_=offset.partition_broadcast(P))
-        nc.sync.dma_start(out=rate_bc[:], in_=rate.partition_broadcast(P))
         load_x(*X_LOADS[3])
 
         def permute_mix(g):
@@ -101,11 +105,32 @@ def tile_aerosol_albedo_heating_h1_kernel(
 
         def cast_vectors():
             nc.scalar.copy(out=vec_rows[0:GF, :, :], in_=vec_raw[0:GF, :].rearrange("r (p t) -> r t p", t=4))
-            nc.scalar.copy(out=vec_rows[32 : 32 + NT, 0, :], in_=vec_raw[32 : 32 + NT, 0:P])
 
         def turn_vectors():
             for t in range(4):
                 nc.tensor.transpose(consts[:, t, :], vec_rows[:, t, :], ident[:])
+
+        turned, spread_ps = {}, {}
+
+        def cast_mu():
+            nc.scalar.copy(out=rows2[0:NT, :], in_=mu_raw[0:NT, :])
+
+        def turn_columns():
+            turned[0] = psum.tile([P, P], F32, name="conv", tag="conv", bufs=2)
+            nc.tensor.transpose(turned[0][:], rows2[:], ident[:])
+
+        def copy_columns():
+            nc.scalar.copy(out=cols2[:], in_=turned[0][:, 0:68])
+
+        def spread(col0):
+            spread_ps[col0] = psum.tile([P, 4, P], F32, name="turn", tag="turn", bufs=2)
+            for j in range(4):
+                nc.tensor.transpose(
+                    spread_ps[col0][:, j, :], cols2[:, col0 + j : col0 + j + 1].to_broadcast([P, P]), ident[:]
+                )
+
+        def spread_exit(dst, col0):
+            nc.scalar.copy(out=dst[:].bitcast(F32), in_=spread_ps[col0][:].rearrange("p j w -> p (j w)"))
 
         xt_ps = {}
         depth_ps, ex, h_bf, codes, scales = {}, {}, {}, {}, {}
@@ -198,7 +223,7 @@ def tile_aerosol_albedo_heating_h1_kernel(
             nc.vector.scalar_tensor_tensor(
                 out=tmp[i][:, cols],
                 in0=conv_ps[i, s][:],
-                scalar=consts[:, 0, 32 + i : 33 + i],
+                scalar=cols2[:, i : i + 1],
                 in1=offset_bc[:, cols],
                 op0=ALU.mult,
                 op1=ALU.add,
@@ -320,6 +345,7 @@ def tile_aerosol_albedo_heating_h1_kernel(
         atten(0, 0, 1)
         depth(0, 1, 1)
         atten(0, 1, 0)
+        cast_mu()
         permute_mix(2)
         depth(0, 2, 0)
         quant(-1, GF, GF + 1)
@@ -334,10 +360,17 @@ def tile_aerosol_albedo_heating_h1_kernel(
             depth(k, 2, 1)
             conv(b, 1)
             atten(k, 1, 1)
+            if k == 1:
+                spread_exit(offset_bc, 32)
             y_round(a - 1)
             atten(k, 2, 0)
+            if k == 1:
+                spread_exit(rate_bc, 64)
             atten(k, 2, 1)
             depth(k + 1, 0, 0)
+            if k == 0:
+                turn_columns()
+                copy_columns()
             times_flux(k, 0, 1)
             sunlit(b, 0)
             sunlit(b, 1)
@@ -355,6 +388,8 @@ def tile_aerosol_albedo_heating_h1_kernel(
                 x_exit(c)
             conv(b + 1, 0)
             depth(k + 1, 0, 1)
+            if k == 0:
+                spread(32)
             conv(b + 1, 1)
             atten(k + 1, 0, 1)
             y_turn(a)
@@ -362,6 +397,8 @@ def tile_aerosol_albedo_heating_h1_kernel(
             y_exit(a)
             atten(k + 1, 1, 0)
             depth(k + 1, 1, 1)
+            if k == 0:
+                spread(64)
             depth(k + 1, 2, 0)
             if k == 0:
                 times_flux(k, 1, 2)

@@ -23,8 +23,9 @@ NT = M // P
 GF = F // 512
 GN = N // 512
 X_LOADS = [(0, 1), (1, 2), (2, 4), (4, 8)]
-X_AT = {0: [2], 1: [3, 4], 2: [5], 4: [6], 5: [7]}
-LATE = 3
+X_MID = {0: [2], 1: [3]}
+X_END = {1: [4], 2: [5], 3: [6], 4: [7]}
+LATE = 4
 
 
 def tile_aerosol_albedo_heating_h1_kernel(
@@ -43,35 +44,32 @@ def tile_aerosol_albedo_heating_h1_kernel(
         rows2 = keep.tile([P, P], F32, name="rows2")
         cols2 = keep.tile([P, 68], F32, name="cols2")
         vec_rows = keep.tile([P, 4, P], F32, name="vec_rows")
-        warm = keep.tile([P, 8], F32, name="warm")
-        mix_sc_raw = keep.tile([P, F], U8, name="mix_sc_raw", align_bytes=64)
-        mix_w_raw = [keep.tile([P, 1024], U8, name="mix_w_raw0"), keep.tile([P, 2048], U8, name="mix_w_raw1")]
-        mix_w = keep.tile([P, GF, 4, 256], U8, name="mix_w", align_bytes=64)
-        mix_sc = keep.tile([P, GF, 4, P], U8, name="mix_sc", align_bytes=64)
-        resp_w = keep.tile([P, GF, 2 * N], U8, name="resp_w", align_bytes=64)
-        resp_sc = keep.tile([P, GF, N], U8, name="resp_sc", align_bytes=64)
+        mix_sc_raw = keep.tile([P, F], U8, name="mix_sc_raw", align_bytes=256)
+        mix_w_raw = [keep.tile([P, 1024], U8, name="mix_w_raw0", align_bytes=256), keep.tile([P, 2048], U8, name="mix_w_raw1", align_bytes=256)]
+        mix_w = keep.tile([P, GF, 4, 256], U8, name="mix_w", align_bytes=256)
+        mix_sc = keep.tile([P, GF, 4, P], U8, name="mix_sc", align_bytes=256)
+        resp_w = keep.tile([P, GF, 2 * N], U8, name="resp_w", align_bytes=256)
+        resp_sc = keep.tile([P, GF, N], U8, name="resp_sc", align_bytes=256)
         offset_bc = keep.tile([P, N], BF16, name="offset_bc")
         rate_bc = keep.tile([P, N], BF16, name="rate_bc")
-        y_sc = keep.tile([P, NCH - LATE, GN, CH], U8, name="y_sc", align_bytes=64)
-        y_sc_last = keep.tile([P, GN, LATE * CH], U8, name="y_sc_last", align_bytes=64)
-        consts = psum.tile([P, 4, P], F32, name="consts")
+        y_sc = keep.tile([P, NCH - LATE, GN, CH], U8, name="y_sc", align_bytes=256)
+        y_sc_last = keep.tile([P, GN, LATE * CH], U8, name="y_sc_last", align_bytes=256)
+        consts = psum.tile([P, P, 4], F32, name="consts")
 
         x_sb = {}
 
         def load_x(c0, c1):
-            t = keep.tile([P, 2 * (c1 - c0), K], BF16, name="x%d" % c0)
+            t = keep.tile([P, 2 * (c1 - c0), K], BF16, name="x%d" % c0, align_bytes=256)
             nc.sync.dma_start(out=t[:], in_=dtau[CH * c0 : CH * c1, :].rearrange("(j p) k -> p j k", p=P))
             for c in range(c0, c1):
                 x_sb[c] = t[:, 2 * (c - c0) : 2 * (c - c0) + 2, :]
 
         nc.vector.memset(mix_sc_raw[:].bitcast(I32), 0)
-        nc.vector.memset(warm[:], 0.0)
         nc.vector.memset(resp_sc[:].rearrange("p g n -> p (g n)").bitcast(I32), 0)
         nc.gpsimd.dma_start(out=vec_raw[0:GF, :], in_=flux.rearrange("(g k) -> g k", g=GF))
-        nc.scalar.activation(out=warm[:, 4:8], in_=warm[:, 0:4], func=ACT.Exp)
         make_identity(nc, ident[:])
+        nc.scalar.activation(out=rows2[:], in_=ident[:], func=ACT.Copy, scale=0.0)
         nc.gpsimd.memset(vec_rows[:], 0.0)
-        nc.gpsimd.memset(rows2[:], 0.0)
 
         load_x(*X_LOADS[0])
         nc.sync.dma_start(out=mix_w_raw[0][:].bitcast(I32), in_=mix_words[0, :, 0:1024].bitcast(I32))
@@ -108,7 +106,7 @@ def tile_aerosol_albedo_heating_h1_kernel(
 
         def turn_vectors():
             for t in range(4):
-                nc.tensor.transpose(consts[:, t, :], vec_rows[:, t, :], ident[:])
+                nc.tensor.transpose(consts[:, :, t], vec_rows[:, t, :], ident[:])
 
         turned, spread_ps = {}, {}
 
@@ -145,7 +143,7 @@ def tile_aerosol_albedo_heating_h1_kernel(
 
         def operand_tiles(c):
             if c not in h_bf:
-                h_bf[c] = work.tile([P, GF + 1, CH * 4], BF16, name="h_bf", tag="h_bf", bufs=5, align_bytes=64)
+                h_bf[c] = work.tile([P, GF + 1, CH * 4], BF16, name="h_bf", tag="h_bf", bufs=5, align_bytes=256)
             return h_bf[c]
 
         def x_exit(c, on_vector=False):
@@ -156,8 +154,8 @@ def tile_aerosol_albedo_heating_h1_kernel(
 
         def quant(c, g0, g1):
             if c not in codes:
-                codes[c] = work.tile([P, (GF + 1) * CH], U32, name="codes", tag="codes", bufs=4, align_bytes=64)
-                scales[c] = work.tile([P, (GF + 1) * CH], U8, name="scales", tag="scales", bufs=4, align_bytes=64)
+                codes[c] = work.tile([P, (GF + 1) * CH], U32, name="codes", tag="codes", bufs=4, align_bytes=256)
+                scales[c] = work.tile([P, (GF + 1) * CH], U8, name="scales", tag="scales", bufs=4, align_bytes=256)
             nc.vector.quantize_mx(
                 out=codes[c][:, CH * g0 : CH * g1].bitcast(FP8X4),
                 scales=scales[c][:, CH * g0 : CH * g1],
@@ -193,16 +191,17 @@ def tile_aerosol_albedo_heating_h1_kernel(
             nc.vector.tensor_tensor(
                 out=operand_tiles(c)[:, g0:g1, :].rearrange("p g (m u e) -> p g m u e", u=2, e=2),
                 in0=ex[c][:, :, g0:g1, :, :].rearrange("p u g m e -> p g m u e"),
-                in1=consts[:, :, g0:g1].rearrange("p (u e) g -> p g u e", u=2).unsqueeze(2).to_broadcast(shape),
+                in1=consts[:, g0:g1, :].rearrange("p g (u e) -> p g u e", u=2).unsqueeze(2).to_broadcast(shape),
                 op=ALU.mult,
             )
 
-        def conv(i, s, tag="conv", bufs=2):
+        def conv(i, s, tag="conv", bufs=2, g0=0, g1=GF):
             if not 0 <= i < NT:
                 return
             c, j = divmod(i, 2)
-            conv_ps[i, s] = psum.tile([P, 512], F32, name="conv", tag=tag, bufs=bufs)
-            for g in range(GF):
+            if g0 == 0:
+                conv_ps[i, s] = psum.tile([P, 512], F32, name="conv", tag=tag, bufs=bufs)
+            for g in range(g0, g1):
                 cols = slice(CH * g + P * j, CH * g + P * (j + 1))
                 nc.tensor.matmul_mx(
                     out=conv_ps[i, s][:],
@@ -233,7 +232,7 @@ def tile_aerosol_albedo_heating_h1_kernel(
             if not 0 <= i < NT:
                 return
             if i not in y:
-                y[i] = work.tile([P, N], F32, name="y", tag="y", bufs=4)
+                y[i] = work.tile([P, N], F32, name="y", tag="y", bufs=4, align_bytes=256)
             cols = slice(512 * s0, 512 * s1)
             eng.tensor_tensor(out=y[i][:, cols], in0=tmp[i][:, cols], in1=rate_bc[:, cols], op=ALU.mult)
 
@@ -243,12 +242,12 @@ def tile_aerosol_albedo_heating_h1_kernel(
             cols = slice(512 * s0, 512 * s1)
             nc.sync.dma_start(out=out_0[P * i : P * (i + 1), cols], in_=y[i][:, cols])
 
-        def y_round(i, s0=0, s1=GN):
+        def y_round(i, s0=0, s1=GN, on_vector=False):
             if not 0 <= i < NT:
                 return
             if i not in y_bf:
                 y_bf[i] = work.tile([P, 2, GN, P, 2], BF16, name="y_bf", tag="y_bf", bufs=4)
-            nc.scalar.copy(
+            (nc.vector.tensor_copy if on_vector else nc.scalar.copy)(
                 out=y_bf[i][:, :, s0:s1, :, :],
                 in_=y[i][:, 512 * s0 : 512 * s1].rearrange("p (s q u e) -> p u s q e", q=P, u=2, e=2),
             )
@@ -278,7 +277,7 @@ def tile_aerosol_albedo_heating_h1_kernel(
                 return
             c, j = divmod(i, 2)
             if c not in yt_sb:
-                yt_sb[c] = work.tile([P, GN, CH * 4], BF16, name="yt_sb", tag="yt_sb", bufs=3, align_bytes=64)
+                yt_sb[c] = work.tile([P, GN, CH * 4], BF16, name="yt_sb", tag="yt_sb", bufs=3, align_bytes=256)
             (nc.vector.tensor_copy if on_vector else nc.scalar.copy)(
                 out=yt_sb[c][:, s0:s1, 512 * j : 512 * (j + 1)].bitcast(F32).rearrange("p s (r u) -> p s r u", u=2),
                 in_=yt_ps[i, s0][:].rearrange("p s u r -> p s r u"),
@@ -290,7 +289,7 @@ def tile_aerosol_albedo_heating_h1_kernel(
             if not 0 <= c < NCH:
                 return
             if c not in y_codes:
-                y_codes[c] = work.tile([P, GN, CH], U32, name="y_codes", tag="y_codes", bufs=3, align_bytes=64)
+                y_codes[c] = work.tile([P, GN, CH], U32, name="y_codes", tag="y_codes", bufs=NCH, align_bytes=256)
             if c < NCH - LATE:
                 nc.vector.quantize_mx(
                     out=y_codes[c][:].rearrange("p s m -> p (s m)").bitcast(FP8X4),
@@ -334,8 +333,8 @@ def tile_aerosol_albedo_heating_h1_kernel(
         x_turn(1)
         permute_mix(0)
         quant(-2, GF, GF + 1)
-        cast_vectors()
         x_exit(1)
+        cast_vectors()
         depth(0, 0, 0)
         depth(0, 0, 1)
         permute_mix(1)
@@ -346,71 +345,88 @@ def tile_aerosol_albedo_heating_h1_kernel(
         depth(0, 1, 1)
         atten(0, 1, 0)
         cast_mu()
+        quant(-1, GF, GF + 1)
         permute_mix(2)
         depth(0, 2, 0)
-        quant(-1, GF, GF + 1)
+        atten(0, 1, 1)
+        depth(0, 2, 1)
         for k in range(NCH):
             a, b = 2 * k - 3, 2 * k - 2
-            sunlit(a, 1)
-            y_quant(k - 3)
-            store_codes(k - 3)
+            last = k == NCH - 1
             times_rate(a)
             store_y(a)
             conv(b, 0)
-            depth(k, 2, 1)
             conv(b, 1)
-            atten(k, 1, 1)
+            y_round(a - 1)
+            for c in X_END.get(k - 1, []):
+                x_exit(c)
             if k == 1:
                 spread_exit(offset_bc, 32)
-            y_round(a - 1)
             atten(k, 2, 0)
+            y_exit(a - 2)
             if k == 1:
                 spread_exit(rate_bc, 64)
             atten(k, 2, 1)
-            depth(k + 1, 0, 0)
             if k == 0:
                 turn_columns()
-                copy_columns()
-            times_flux(k, 0, 1)
+            if k < 2:
+                times_flux(k, 0, 1)
+                times_flux(k, 1, 2)
+            else:
+                times_flux(k, 0, 2)
             sunlit(b, 0)
+            if last:
+                y_quant(k - 3, 0, 1)
+            else:
+                y_quant(k - 3)
+                store_codes(k - 3)
+            times_rate(b, 0, 1)
             sunlit(b, 1)
-            times_rate(b)
-            if k == NCH - 1:
+            times_rate(b, 1, 2)
+            if k == NCH - 2:
                 store_early_scales()
             store_y(b)
-            y_turn(a - 1)
-            for c in X_AT.get(k, []):
+            for c in X_MID.get(k, []):
                 x_turn(c)
+            depth(k + 1, 0, 0)
+            depth(k + 1, 0, 1)
+            y_turn(a - 1)
             atten(k + 1, 0, 0)
+            if k == 0:
+                copy_columns()
+            for c in X_MID.get(k, []):
+                x_exit(c)
             y_exit(a - 1)
             y_round(a)
-            for c in X_AT.get(k, []):
-                x_exit(c)
+            atten(k + 1, 0, 1)
             conv(b + 1, 0)
-            depth(k + 1, 0, 1)
+            conv(b + 1, 1)
+            depth(k + 1, 1, 0)
+            depth(k + 1, 1, 1)
+            y_turn(a)
             if k == 0:
                 spread(32)
-            conv(b + 1, 1)
-            atten(k + 1, 0, 1)
-            y_turn(a)
-            depth(k + 1, 1, 0)
-            y_exit(a)
-            atten(k + 1, 1, 0)
-            depth(k + 1, 1, 1)
-            if k == 0:
                 spread(64)
+            for c in X_END.get(k, []):
+                x_turn(c)
+            atten(k + 1, 1, 0)
+            atten(k + 1, 1, 1)
             depth(k + 1, 2, 0)
-            if k == 0:
-                times_flux(k, 1, 2)
-                times_flux(k, 2, 3)
-            else:
-                times_flux(k, 1, 3)
+            depth(k + 1, 2, 1)
+            times_flux(k, 2, 3)
             sunlit(b + 1, 0)
             if k < NCH - 2:
+                sunlit(b + 1, 1)
                 quant(k, 0, GF + 1)
-            else:
+            elif not last:
                 quant(k, 0, 2)
+                sunlit(b + 1, 1)
                 quant(k, 2, 3)
+        y_exit(11)
+        quant(7, 0, 2)
+        quant(7, 2, 3)
+        y_quant(4, 1, 2)
+        store_codes(4)
         y_quant(5)
         store_codes(5)
         sunlit(13, 1)
@@ -421,41 +437,41 @@ def tile_aerosol_albedo_heating_h1_kernel(
         y_round(12)
         conv(14, 0, "depth", 3)
         conv(14, 1, "depth", 3)
-        y_turn(12)
-        conv(15, 0, "depth", 3)
+        conv(15, 0)
         conv(15, 1)
+        y_turn(12)
         sunlit(14, 0)
         sunlit(14, 1)
         sunlit(15, 0)
         sunlit(15, 1)
-        y_exit(12)
         y_round(13, 1, 2)
+        y_exit(12)
         y_round(13, 0, 1)
         y_turn(13)
-        times_rate(14, 0, 1)
+        times_rate(14, 0, 1, nc.vector)
         store_y(14, 0, 1)
         times_rate(14, 1, 2, nc.vector)
         store_y(14, 1, 2)
-        y_exit(13)
         y_round(14, 0, 1)
+        y_exit(13)
         y_round(14, 1, 2)
         times_rate(15, 0, 1, nc.vector)
         store_y(15, 0, 1)
-        y_round_direct(15, 1)
         times_rate(15, 1, 2, nc.vector)
         store_y(15, 1, 2)
-        y_round(15, 0, 1)
+        y_round(15, 0, 1, True)
+        y_round(15, 1, 2, True)
         y_quant(6)
         store_codes(6)
-        y_turn(15, 1, 2, "depth", 3)
         y_turn(14)
+        y_turn(15, 1, 2, "depth", 3)
         y_turn(15, 0, 1, "depth", 3)
-        y_exit(15, 1, 2, on_vector=True)
         y_exit(14)
-        y_exit(15, 0, 1, on_vector=True)
-        y_quant(7, 1, 2, 1, 2)
+        y_exit(15, 1, 2, on_vector=True)
+        y_exit(15, 0, 1)
         y_quant(7, 0, 2, 0, 1)
         store_codes(7, 0, 2, 0, 1)
+        y_quant(7, 1, 2, 1, 2)
         y_quant(7, 0, 1, 1, 2)
         store_codes(7, 0, 2, 1, 2)
         store_scales(M - LATE * CH, M, y_sc_last, [nc.scalar, nc.sync, nc.scalar, nc.sync])

@@ -17,15 +17,27 @@ ALU = mybir.AluOpType
 ACT = mybir.ActivationFunctionType
 
 P = 128
-CH = 256
-NCH = M // CH
-NT = M // P
-GF = F // 512
-GN = N // 512
-X_LOADS = [(0, 1), (1, 2), (2, 4), (4, 8)]
-X_MID = {0: [2], 1: [3]}
-X_END = {1: [4], 2: [5], 3: [6], 4: [7]}
+GROUP = 512
+CHUNK = 256
+CHUNKS = M // CHUNK
+TILES = M // P
+BAND_GROUPS = F // GROUP
+LEVEL_GROUPS = N // GROUP
+ALIGN = 256
+
+BANKS = {"depth": 3, "conv": 2, "turn": 2}
+
+AHEAD = 2
+DTAU_SLOT = BAND_GROUPS
+DTAU_LOADS = [(0, 1), (1, 2), (2, 4), (4, CHUNKS)]
+TURN_MID = {0: 2, 1: 3}
+TURN_END = {1: 4, 2: 5, 3: 6, 4: 7}
+PLANES_LAG = 3
 LATE = 4
+EARLY = CHUNKS - LATE
+
+OFFSET_ROW, RATE_ROW = 32, 64
+PAIR_ROWS = N // (2 * P)
 
 
 def tile_aerosol_albedo_heating_h1_kernel(
@@ -38,440 +50,451 @@ def tile_aerosol_albedo_heating_h1_kernel(
         psum = ctx.enter_context(tc.psum_pool(name="psum", bufs=1))
         ctx.enter_context(tc.manual_schedule())
 
+        def bank(role, shape):
+            return psum.tile(shape, F32, name=role, tag=role, bufs=BANKS[role])
+
+        def levels(s0, s1):
+            return slice(GROUP * s0, GROUP * s1)
+
         ident = keep.tile([P, P], F32, name="ident")
-        vec_raw = keep.tile([P, 512], BF16, name="vec_raw")
+        flux_raw = keep.tile([P, GROUP], BF16, name="flux_raw")
         mu_raw = keep.tile([P, P], BF16, name="mu_raw")
-        rows2 = keep.tile([P, P], F32, name="rows2")
-        cols2 = keep.tile([P, 68], F32, name="cols2")
-        vec_rows = keep.tile([P, 4, P], F32, name="vec_rows")
-        mix_sc_raw = keep.tile([P, F], U8, name="mix_sc_raw", align_bytes=256)
-        mix_w_raw = [keep.tile([P, 1024], U8, name="mix_w_raw0", align_bytes=256), keep.tile([P, 2048], U8, name="mix_w_raw1", align_bytes=256)]
-        mix_w = keep.tile([P, GF, 4, 256], U8, name="mix_w", align_bytes=256)
-        mix_sc = keep.tile([P, GF, 4, P], U8, name="mix_sc", align_bytes=256)
-        resp_w = keep.tile([P, GF, 2 * N], U8, name="resp_w", align_bytes=256)
-        resp_sc = keep.tile([P, GF, N], U8, name="resp_sc", align_bytes=256)
-        offset_bc = keep.tile([P, N], BF16, name="offset_bc")
-        rate_bc = keep.tile([P, N], BF16, name="rate_bc")
-        y_sc = keep.tile([P, NCH - LATE, GN, CH], U8, name="y_sc", align_bytes=256)
-        y_sc_last = keep.tile([P, GN, LATE * CH], U8, name="y_sc_last", align_bytes=256)
-        consts = psum.tile([P, P, 4], F32, name="consts")
+        vec_rows = keep.tile([P, P], F32, name="vec_rows")
+        vec_cols = keep.tile([P, RATE_ROW + PAIR_ROWS], F32, name="vec_cols")
+        flux_rows = keep.tile([P, 4, P], F32, name="flux_rows")
+        mix_sc_raw = keep.tile([P, F], U8, name="mix_sc_raw", align_bytes=ALIGN)
+        mix_w_first = keep.tile([P, 2 * GROUP], U8, name="mix_w_first", align_bytes=ALIGN)
+        mix_w_rest = keep.tile([P, 2 * (F - GROUP)], U8, name="mix_w_rest", align_bytes=ALIGN)
+        mix_w = keep.tile([P, BAND_GROUPS, 4, 2 * P], U8, name="mix_w", align_bytes=ALIGN)
+        mix_sc = keep.tile([P, BAND_GROUPS, 4, P], U8, name="mix_sc", align_bytes=ALIGN)
+        resp_w = keep.tile([P, BAND_GROUPS, 2 * N], U8, name="resp_w", align_bytes=ALIGN)
+        resp_sc = keep.tile([P, BAND_GROUPS, N], U8, name="resp_sc", align_bytes=ALIGN)
+        offset_all = keep.tile([P, N], BF16, name="offset_all")
+        rate_all = keep.tile([P, N], BF16, name="rate_all")
+        y_sc_early = keep.tile([P, EARLY, LEVEL_GROUPS, CHUNK], U8, name="y_sc_early", align_bytes=ALIGN)
+        y_sc_late = keep.tile([P, LEVEL_GROUPS, LATE * CHUNK], U8, name="y_sc_late", align_bytes=ALIGN)
+        flux_ps = psum.tile([P, P, 4], F32, name="flux_ps")
 
-        x_sb = {}
+        dtau_sb = {}
 
-        def load_x(c0, c1):
-            t = keep.tile([P, 2 * (c1 - c0), K], BF16, name="x%d" % c0, align_bytes=256)
-            nc.sync.dma_start(out=t[:], in_=dtau[CH * c0 : CH * c1, :].rearrange("(j p) k -> p j k", p=P))
+        def load_dtau(c0, c1):
+            rows = keep.tile([P, 2 * (c1 - c0), K], BF16, name="dtau%d" % c0, align_bytes=ALIGN)
+            nc.sync.dma_start(out=rows[:], in_=dtau[CHUNK * c0 : CHUNK * c1, :].rearrange("(j p) k -> p j k", p=P))
             for c in range(c0, c1):
-                x_sb[c] = t[:, 2 * (c - c0) : 2 * (c - c0) + 2, :]
+                dtau_sb[c] = rows[:, 2 * (c - c0) : 2 * (c - c0) + 2, :]
 
         nc.vector.memset(mix_sc_raw[:].bitcast(I32), 0)
         nc.vector.memset(resp_sc[:].rearrange("p g n -> p (g n)").bitcast(I32), 0)
-        nc.gpsimd.dma_start(out=vec_raw[0:GF, :], in_=flux.rearrange("(g k) -> g k", g=GF))
+        nc.gpsimd.dma_start(out=flux_raw[0:BAND_GROUPS, :], in_=flux.rearrange("(g k) -> g k", g=BAND_GROUPS))
         make_identity(nc, ident[:])
-        nc.scalar.activation(out=rows2[:], in_=ident[:], func=ACT.Copy, scale=0.0)
-        nc.gpsimd.memset(vec_rows[:], 0.0)
+        nc.scalar.activation(out=vec_rows[:], in_=ident[:], func=ACT.Copy, scale=0.0)
+        nc.gpsimd.memset(flux_rows[:], 0.0)
 
-        load_x(*X_LOADS[0])
-        nc.sync.dma_start(out=mix_w_raw[0][:].bitcast(I32), in_=mix_words[0, :, 0:1024].bitcast(I32))
+        load_dtau(*DTAU_LOADS[0])
+        nc.sync.dma_start(out=mix_w_first[:].bitcast(I32), in_=mix_words[0, :, 0 : 2 * GROUP].bitcast(I32))
         for q in range(4):
             nc.sync.dma_start(
                 out=mix_sc_raw[32 * q : 32 * q + 4, :].bitcast(I32), in_=mix_scales[0, 4 * q : 4 * q + 4, :].bitcast(I32)
             )
-        load_x(*X_LOADS[1])
-        nc.sync.dma_start(out=mix_w_raw[1][:].bitcast(I32), in_=mix_words[0, :, 1024:3072].bitcast(I32))
-        load_x(*X_LOADS[2])
-        nc.sync.dma_start(out=mu_raw[0:NT, :], in_=mu0.rearrange("(i p) -> i p", p=P))
-        nc.sync.dma_start(out=rows2[32:36, :].bitcast(I32), in_=offset.rearrange("(j w) -> j w", j=4).bitcast(I32))
-        nc.sync.dma_start(out=rows2[64:68, :].bitcast(I32), in_=rate.rearrange("(j w) -> j w", j=4).bitcast(I32))
+        load_dtau(*DTAU_LOADS[1])
+        nc.sync.dma_start(out=mix_w_rest[:].bitcast(I32), in_=mix_words[0, :, 2 * GROUP : 2 * F].bitcast(I32))
+        load_dtau(*DTAU_LOADS[2])
+        nc.sync.dma_start(out=mu_raw[0:TILES, :], in_=mu0.rearrange("(i p) -> i p", p=P))
+        for vec, row in ((offset, OFFSET_ROW), (rate, RATE_ROW)):
+            nc.sync.dma_start(
+                out=vec_rows[row : row + PAIR_ROWS, :].bitcast(I32),
+                in_=vec.rearrange("(j w) -> j w", j=PAIR_ROWS).bitcast(I32),
+            )
         nc.sync.dma_start(out=resp_w[:].bitcast(I32), in_=resp_words.rearrange("g p b -> p g b").bitcast(I32))
         for q in range(4):
             nc.sync.dma_start(
                 out=resp_sc[32 * q : 32 * q + 4, :, :].bitcast(I32),
                 in_=resp_scales[:, 4 * q : 4 * q + 4, :].rearrange("g r n -> r g n").bitcast(I32),
             )
-        load_x(*X_LOADS[3])
+        load_dtau(*DTAU_LOADS[3])
 
-        def permute_mix(g):
-            src = mix_w_raw[0][:] if g == 0 else mix_w_raw[1][:, 1024 * (g - 1) : 1024 * g]
+        def reorder_mix(g):
+            words = mix_w_first[:] if g == 0 else mix_w_rest[:, 2 * GROUP * (g - 1) : 2 * GROUP * g]
             nc.vector.tensor_copy(
                 out=mix_w[:, g, :, :].rearrange("p t (m b) -> p t m b", b=2),
-                in_=src.rearrange("p (m t b) -> p t m b", t=4, b=2),
+                in_=words.rearrange("p (m t b) -> p t m b", t=4, b=2),
             )
             nc.vector.tensor_copy(
-                out=mix_sc[:, g, :, :], in_=mix_sc_raw[:, 512 * g : 512 * (g + 1)].rearrange("p (m t) -> p t m", t=4)
+                out=mix_sc[:, g, :, :],
+                in_=mix_sc_raw[:, GROUP * g : GROUP * (g + 1)].rearrange("p (m t) -> p t m", t=4),
             )
 
-        def cast_vectors():
-            nc.scalar.copy(out=vec_rows[0:GF, :, :], in_=vec_raw[0:GF, :].rearrange("r (p t) -> r t p", t=4))
+        def cast_flux():
+            nc.scalar.copy(
+                out=flux_rows[0:BAND_GROUPS, :, :], in_=flux_raw[0:BAND_GROUPS, :].rearrange("g (p t) -> g t p", t=4)
+            )
 
-        def turn_vectors():
+        def turn_flux():
             for t in range(4):
-                nc.tensor.transpose(consts[:, :, t], vec_rows[:, t, :], ident[:])
-
-        turned, spread_ps = {}, {}
+                nc.tensor.transpose(flux_ps[:, :, t], flux_rows[:, t, :], ident[:])
 
         def cast_mu():
-            nc.scalar.copy(out=rows2[0:NT, :], in_=mu_raw[0:NT, :])
+            nc.scalar.copy(out=vec_rows[0:TILES, :], in_=mu_raw[0:TILES, :])
 
-        def turn_columns():
-            turned[0] = psum.tile([P, P], F32, name="conv", tag="conv", bufs=2)
-            nc.tensor.transpose(turned[0][:], rows2[:], ident[:])
+        def turn_vectors():
+            turned = bank("conv", [P, P])
+            nc.tensor.transpose(turned[:], vec_rows[:], ident[:])
+            return turned
 
-        def copy_columns():
-            nc.scalar.copy(out=cols2[:], in_=turned[0][:, 0:68])
+        def copy_vectors(turned):
+            nc.scalar.copy(out=vec_cols[:], in_=turned[:, 0 : RATE_ROW + PAIR_ROWS])
 
-        def spread(col0):
-            spread_ps[col0] = psum.tile([P, 4, P], F32, name="turn", tag="turn", bufs=2)
-            for j in range(4):
-                nc.tensor.transpose(
-                    spread_ps[col0][:, j, :], cols2[:, col0 + j : col0 + j + 1].to_broadcast([P, P]), ident[:]
+        def spread(row, role):
+            pairs = bank(role, [P, PAIR_ROWS, P])
+            for j in range(PAIR_ROWS):
+                nc.tensor.transpose(pairs[:, j, :], vec_cols[:, row + j : row + j + 1].to_broadcast([P, P]), ident[:])
+            return pairs[:].rearrange("p j w -> p (j w)")
+
+        dtau_ps, depth_ps, decay, unquantised, codes, scales = {}, {}, {}, {}, {}, {}
+
+        def slots(c):
+            if c not in unquantised:
+                unquantised[c] = work.tile(
+                    [P, BAND_GROUPS + 1, CHUNK * 4], BF16, name="unquantised", tag="unquantised", bufs=5, align_bytes=ALIGN
                 )
+            return unquantised[c]
 
-        def spread_exit(dst, col0):
-            nc.scalar.copy(out=dst[:].bitcast(F32), in_=spread_ps[col0][:].rearrange("p j w -> p (j w)"))
-
-        xt_ps = {}
-        depth_ps, ex, h_bf, codes, scales = {}, {}, {}, {}, {}
-        conv_ps, tmp, y, y_bf, yt_ps, yt_sb = {}, {}, {}, {}, {}, {}
-
-        def x_turn(c):
-            xt_ps[c] = psum.tile([P, 2, 2, P], F32, name="turn", tag="turn", bufs=2)
+        def dtau_turn(c):
+            dtau_ps[c] = bank("turn", [P, 2, 2, P])
             for j in range(2):
-                words = x_sb[c][:, j, :].bitcast(F32)
+                pairs = dtau_sb[c][:, j, :].bitcast(F32)
                 for u in range(2):
-                    nc.tensor.transpose(xt_ps[c][:, j, u, :], words[:, u:256:2], ident[:])
+                    nc.tensor.transpose(dtau_ps[c][:, j, u, :], pairs[:, u : K // 2 : 2], ident[:])
 
-        def operand_tiles(c):
-            if c not in h_bf:
-                h_bf[c] = work.tile([P, GF + 1, CH * 4], BF16, name="h_bf", tag="h_bf", bufs=5, align_bytes=256)
-            return h_bf[c]
-
-        def x_exit(c, on_vector=False):
-            (nc.vector.tensor_copy if on_vector else nc.scalar.copy)(
-                out=operand_tiles(c - 2)[:, GF, :].bitcast(F32).rearrange("p (j r u) -> p j r u", j=2, u=2),
-                in_=xt_ps[c][:].rearrange("p j u r -> p j r u"),
+        def dtau_exit(c):
+            nc.scalar.copy(
+                out=slots(c - AHEAD)[:, DTAU_SLOT, :].bitcast(F32).rearrange("p (j r u) -> p j r u", j=2, u=2),
+                in_=dtau_ps[c][:].rearrange("p j u r -> p j r u"),
             )
 
-        def quant(c, g0, g1):
+        def quantise(c, slot0, slot1):
             if c not in codes:
-                codes[c] = work.tile([P, (GF + 1) * CH], U32, name="codes", tag="codes", bufs=4, align_bytes=256)
-                scales[c] = work.tile([P, (GF + 1) * CH], U8, name="scales", tag="scales", bufs=4, align_bytes=256)
+                width = (BAND_GROUPS + 1) * CHUNK
+                codes[c] = work.tile([P, width], U32, name="codes", tag="codes", bufs=4, align_bytes=ALIGN)
+                scales[c] = work.tile([P, width], U8, name="scales", tag="scales", bufs=4, align_bytes=ALIGN)
             nc.vector.quantize_mx(
-                out=codes[c][:, CH * g0 : CH * g1].bitcast(FP8X4),
-                scales=scales[c][:, CH * g0 : CH * g1],
-                in_=h_bf[c][:, g0:g1, :].rearrange("p g x -> p (g x)"),
+                out=codes[c][:, CHUNK * slot0 : CHUNK * slot1].bitcast(FP8X4),
+                scales=scales[c][:, CHUNK * slot0 : CHUNK * slot1],
+                in_=unquantised[c][:, slot0:slot1, :].rearrange("p g x -> p (g x)"),
             )
 
         def depth(c, g, u):
-            if not 0 <= c < NCH:
+            if c >= CHUNKS:
                 return
-            depth_ps[c, g, u] = psum.tile([P, 2, CH], F32, name="depth", tag="depth", bufs=3)
+            depth_ps[c, g, u] = bank("depth", [P, 2, CHUNK])
             for e in range(2):
                 nc.tensor.matmul_mx(
                     out=depth_ps[c, g, u][:, e, :],
                     lhsT=mix_w[:, g, 2 * u + e, :].bitcast(FP4X4),
                     lhsT_scale=mix_sc[:, g, 2 * u + e, :],
-                    rhs=codes[c - 2][:, GF * CH :].bitcast(FP8X4),
-                    rhs_scale=scales[c - 2][:, GF * CH :],
+                    rhs=codes[c - AHEAD][:, DTAU_SLOT * CHUNK :].bitcast(FP8X4),
+                    rhs_scale=scales[c - AHEAD][:, DTAU_SLOT * CHUNK :],
                     start=True,
                     stop=True,
                 )
 
-        def atten(c, g, u):
-            if not 0 <= c < NCH:
+        def attenuate(c, g, u):
+            if c >= CHUNKS:
                 return
-            if c not in ex:
-                ex[c] = work.tile([P, 2, GF, CH, 2], F32, name="ex", tag="ex", bufs=2)
+            if c not in decay:
+                decay[c] = work.tile([P, 2, BAND_GROUPS, CHUNK, 2], F32, name="decay", tag="decay", bufs=2)
             nc.scalar.activation(
-                out=ex[c][:, u, g, :, :], in_=depth_ps[c, g, u][:].rearrange("p e m -> p m e"), func=ACT.Exp, scale=-1.0
+                out=decay[c][:, u, g, :, :],
+                in_=depth_ps[c, g, u][:].rearrange("p e m -> p m e"),
+                func=ACT.Exp,
+                scale=-1.0,
             )
 
         def times_flux(c, g0, g1):
-            shape = [P, g1 - g0, CH, 2, 2]
+            shape = [P, g1 - g0, CHUNK, 2, 2]
             nc.vector.tensor_tensor(
-                out=operand_tiles(c)[:, g0:g1, :].rearrange("p g (m u e) -> p g m u e", u=2, e=2),
-                in0=ex[c][:, :, g0:g1, :, :].rearrange("p u g m e -> p g m u e"),
-                in1=consts[:, g0:g1, :].rearrange("p g (u e) -> p g u e", u=2).unsqueeze(2).to_broadcast(shape),
+                out=slots(c)[:, g0:g1, :].rearrange("p g (m u e) -> p g m u e", u=2, e=2),
+                in0=decay[c][:, :, g0:g1, :, :].rearrange("p u g m e -> p g m u e"),
+                in1=flux_ps[:, g0:g1, :].rearrange("p g (u e) -> p g u e", u=2).unsqueeze(2).to_broadcast(shape),
                 op=ALU.mult,
             )
 
-        def conv(i, s, tag="conv", bufs=2, g0=0, g1=GF):
-            if not 0 <= i < NT:
+        conv_ps, sunlit_sb, y, y_pairs, y_ps, y_turned, y_codes = {}, {}, {}, {}, {}, {}, {}
+
+        def conv(i, s, role="conv"):
+            if i < 0:
                 return
             c, j = divmod(i, 2)
-            if g0 == 0:
-                conv_ps[i, s] = psum.tile([P, 512], F32, name="conv", tag=tag, bufs=bufs)
-            for g in range(g0, g1):
-                cols = slice(CH * g + P * j, CH * g + P * (j + 1))
+            conv_ps[i, s] = bank(role, [P, GROUP])
+            for g in range(BAND_GROUPS):
+                scenes = slice(CHUNK * g + P * j, CHUNK * g + P * (j + 1))
                 nc.tensor.matmul_mx(
                     out=conv_ps[i, s][:],
-                    lhsT=codes[c][:, cols].bitcast(FP8X4),
-                    lhsT_scale=scales[c][:, cols],
-                    rhs=resp_w[:, g, 1024 * s : 1024 * (s + 1)].bitcast(FP4X4),
-                    rhs_scale=resp_sc[:, g, 512 * s : 512 * (s + 1)],
+                    lhsT=codes[c][:, scenes].bitcast(FP8X4),
+                    lhsT_scale=scales[c][:, scenes],
+                    rhs=resp_w[:, g, 2 * GROUP * s : 2 * GROUP * (s + 1)].bitcast(FP4X4),
+                    rhs_scale=resp_sc[:, g, levels(s, s + 1)],
                     start=(g == 0),
-                    stop=(g == GF - 1),
+                    stop=(g == BAND_GROUPS - 1),
                 )
 
         def sunlit(i, s):
-            if not 0 <= i < NT:
+            if i < 0:
                 return
-            if i not in tmp:
-                tmp[i] = work.tile([P, N], F32, name="tmp", tag="tmp", bufs=3)
-            cols = slice(512 * s, 512 * (s + 1))
+            if i not in sunlit_sb:
+                sunlit_sb[i] = work.tile([P, N], F32, name="sunlit", tag="sunlit", bufs=3)
             nc.vector.scalar_tensor_tensor(
-                out=tmp[i][:, cols],
+                out=sunlit_sb[i][:, levels(s, s + 1)],
                 in0=conv_ps[i, s][:],
-                scalar=cols2[:, i : i + 1],
-                in1=offset_bc[:, cols],
+                scalar=vec_cols[:, i : i + 1],
+                in1=offset_all[:, levels(s, s + 1)],
                 op0=ALU.mult,
                 op1=ALU.add,
             )
 
-        def times_rate(i, s0=0, s1=GN, eng=nc.gpsimd):
-            if not 0 <= i < NT:
+        def times_rate(i, s0=0, s1=LEVEL_GROUPS, engine=nc.gpsimd, factor=rate_all):
+            if i < 0:
                 return
             if i not in y:
-                y[i] = work.tile([P, N], F32, name="y", tag="y", bufs=4, align_bytes=256)
-            cols = slice(512 * s0, 512 * s1)
-            eng.tensor_tensor(out=y[i][:, cols], in0=tmp[i][:, cols], in1=rate_bc[:, cols], op=ALU.mult)
+                y[i] = work.tile([P, N], F32, name="y", tag="y", bufs=4, align_bytes=ALIGN)
+            cols = levels(s0, s1)
+            engine.tensor_tensor(out=y[i][:, cols], in0=sunlit_sb[i][:, cols], in1=factor[:, cols], op=ALU.mult)
 
-        def store_y(i, s0=0, s1=GN):
-            if not 0 <= i < NT:
+        def store_y(i, s0=0, s1=LEVEL_GROUPS):
+            if i < 0:
                 return
-            cols = slice(512 * s0, 512 * s1)
-            nc.sync.dma_start(out=out_0[P * i : P * (i + 1), cols], in_=y[i][:, cols])
+            nc.sync.dma_start(out=out_0[P * i : P * (i + 1), levels(s0, s1)], in_=y[i][:, levels(s0, s1)])
 
-        def y_round(i, s0=0, s1=GN, on_vector=False):
-            if not 0 <= i < NT:
+        def y_round(i, s0=0, s1=LEVEL_GROUPS, copy=nc.scalar.copy):
+            if i < 0:
                 return
-            if i not in y_bf:
-                y_bf[i] = work.tile([P, 2, GN, P, 2], BF16, name="y_bf", tag="y_bf", bufs=4)
-            (nc.vector.tensor_copy if on_vector else nc.scalar.copy)(
-                out=y_bf[i][:, :, s0:s1, :, :],
-                in_=y[i][:, 512 * s0 : 512 * s1].rearrange("p (s q u e) -> p u s q e", q=P, u=2, e=2),
+            if i not in y_pairs:
+                y_pairs[i] = work.tile([P, 2, LEVEL_GROUPS, P, 2], BF16, name="y_pairs", tag="y_pairs", bufs=4)
+            copy(
+                out=y_pairs[i][:, :, s0:s1, :, :],
+                in_=y[i][:, levels(s0, s1)].rearrange("p (s q u e) -> p u s q e", q=P, u=2, e=2),
             )
 
-        def y_round_direct(i, s):
-            if i not in y_bf:
-                y_bf[i] = work.tile([P, 2, GN, P, 2], BF16, name="y_bf", tag="y_bf", bufs=4)
-            cols = slice(512 * s, 512 * (s + 1))
-            nc.vector.tensor_tensor(
-                out=y_bf[i][:, :, s, :, :],
-                in0=tmp[i][:, cols].rearrange("p (q u e) -> p u q e", u=2, e=2),
-                in1=rate_bc[:, cols].rearrange("p (q u e) -> p u q e", u=2, e=2),
-                op=ALU.mult,
-            )
-
-        def y_turn(i, s0=0, s1=GN, tag="turn", bufs=2):
-            if not 0 <= i < NT:
+        def y_turn(i, s0=0, s1=LEVEL_GROUPS, role="turn"):
+            if i < 0:
                 return
-            yt_ps[i, s0] = psum.tile([P, s1 - s0, 2, P], F32, name="turn", tag=tag, bufs=bufs)
+            y_ps[i, s0] = bank(role, [P, s1 - s0, 2, P])
             for s in range(s0, s1):
                 for u in range(2):
-                    words = y_bf[i][:, u, s, :, :].rearrange("p q e -> p (q e)").bitcast(F32)
-                    nc.tensor.transpose(yt_ps[i, s0][:, s - s0, u, :], words, ident[:])
+                    pairs = y_pairs[i][:, u, s, :, :].rearrange("p q e -> p (q e)").bitcast(F32)
+                    nc.tensor.transpose(y_ps[i, s0][:, s - s0, u, :], pairs, ident[:])
 
-        def y_exit(i, s0=0, s1=GN, on_vector=False):
-            if not 0 <= i < NT:
+        def y_exit(i, s0=0, s1=LEVEL_GROUPS, copy=nc.scalar.copy):
+            if i < 0:
                 return
             c, j = divmod(i, 2)
-            if c not in yt_sb:
-                yt_sb[c] = work.tile([P, GN, CH * 4], BF16, name="yt_sb", tag="yt_sb", bufs=3, align_bytes=256)
-            (nc.vector.tensor_copy if on_vector else nc.scalar.copy)(
-                out=yt_sb[c][:, s0:s1, 512 * j : 512 * (j + 1)].bitcast(F32).rearrange("p s (r u) -> p s r u", u=2),
-                in_=yt_ps[i, s0][:].rearrange("p s u r -> p s r u"),
+            if c not in y_turned:
+                y_turned[c] = work.tile(
+                    [P, LEVEL_GROUPS, CHUNK * 4], BF16, name="y_turned", tag="y_turned", bufs=3, align_bytes=ALIGN
+                )
+            copy(
+                out=y_turned[c][:, s0:s1, 4 * P * j : 4 * P * (j + 1)].bitcast(F32).rearrange("p s (r u) -> p s r u", u=2),
+                in_=y_ps[i, s0][:].rearrange("p s u r -> p s r u"),
             )
 
-        y_codes = {}
-
-        def y_quant(c, s0=0, s1=GN, j0=0, j1=2):
-            if not 0 <= c < NCH:
+        def y_quantise(c, s0=0, s1=LEVEL_GROUPS, j0=0, j1=2):
+            if c < 0:
                 return
             if c not in y_codes:
-                y_codes[c] = work.tile([P, GN, CH], U32, name="y_codes", tag="y_codes", bufs=NCH, align_bytes=256)
-            if c < NCH - LATE:
+                y_codes[c] = work.tile(
+                    [P, LEVEL_GROUPS, CHUNK], U32, name="y_codes", tag="y_codes", bufs=CHUNKS, align_bytes=ALIGN
+                )
+            if c < EARLY:
                 nc.vector.quantize_mx(
                     out=y_codes[c][:].rearrange("p s m -> p (s m)").bitcast(FP8X4),
-                    scales=y_sc[:, c, :, :].rearrange("p s m -> p (s m)"),
-                    in_=yt_sb[c][:].rearrange("p s x -> p (s x)"),
+                    scales=y_sc_early[:, c, :, :].rearrange("p s m -> p (s m)"),
+                    in_=y_turned[c][:].rearrange("p s x -> p (s x)"),
                 )
                 return
-            m0 = CH * (c - NCH + LATE)
+            m0 = CHUNK * (c - EARLY)
             for s in range(s0, s1):
                 nc.vector.quantize_mx(
                     out=y_codes[c][:, s, P * j0 : P * j1].bitcast(FP8X4),
-                    scales=y_sc_last[:, s, m0 + P * j0 : m0 + P * j1],
-                    in_=yt_sb[c][:, s, 512 * j0 : 512 * j1],
+                    scales=y_sc_late[:, s, m0 + P * j0 : m0 + P * j1],
+                    in_=y_turned[c][:, s, 4 * P * j0 : 4 * P * j1],
                 )
 
-        def store_codes(c, s0=0, s1=GN, j0=0, j1=2):
-            if not 0 <= c < NCH:
+        def store_codes(c, j0=0, j1=2):
+            if c < 0:
                 return
+            scenes = slice(CHUNK * c + P * j0, CHUNK * c + P * j1)
             nc.sync.dma_start(
-                out=out_1[s0:s1, :, CH * c + P * j0 : CH * c + P * j1, :].rearrange("g p m t -> p g (m t)").bitcast(I32),
-                in_=y_codes[c][:, s0:s1, P * j0 : P * j1].bitcast(I32),
+                out=out_1[:, :, scenes, :].rearrange("g p m t -> p g (m t)").bitcast(I32),
+                in_=y_codes[c][:, :, P * j0 : P * j1].bitcast(I32),
             )
 
-        def store_scales(m0, m1, src, engs):
-            for q in range(4):
-                engs[q].dma_start(
-                    out=out_2[:, 4 * q : 4 * q + 4, m0:m1].rearrange("g r m -> r g m").bitcast(I32),
-                    in_=src[32 * q : 32 * q + 4, :, :].bitcast(I32),
-                )
-
         def store_early_scales():
-            for s in range(GN):
+            for s in range(LEVEL_GROUPS):
                 for q in range(4):
                     nc.sync.dma_start(
-                        out=out_2[s, 4 * q : 4 * q + 4, 0 : M - LATE * CH].rearrange("r (c m) -> r c m", m=CH).bitcast(I32),
-                        in_=y_sc[32 * q : 32 * q + 4, :, s, :].bitcast(I32),
+                        out=out_2[s, 4 * q : 4 * q + 4, 0 : EARLY * CHUNK].rearrange("r (c m) -> r c m", m=CHUNK).bitcast(I32),
+                        in_=y_sc_early[32 * q : 32 * q + 4, :, s, :].bitcast(I32),
                     )
 
-        x_turn(0)
-        x_exit(0)
-        x_turn(1)
-        permute_mix(0)
-        quant(-2, GF, GF + 1)
-        x_exit(1)
-        cast_vectors()
+        def store_late_scales(c0, c1, queues):
+            for q in range(4):
+                queues[q].dma_start(
+                    out=out_2[:, 4 * q : 4 * q + 4, CHUNK * c0 : CHUNK * c1].rearrange("g r m -> r g m").bitcast(I32),
+                    in_=y_sc_late[32 * q : 32 * q + 4, :, CHUNK * (c0 - EARLY) : CHUNK * (c1 - EARLY)].bitcast(I32),
+                )
+
+        dtau_turn(0)
+        dtau_exit(0)
+        dtau_turn(1)
+        reorder_mix(0)
+        quantise(0 - AHEAD, DTAU_SLOT, DTAU_SLOT + 1)
+        dtau_exit(1)
+        cast_flux()
         depth(0, 0, 0)
         depth(0, 0, 1)
-        permute_mix(1)
+        reorder_mix(1)
         depth(0, 1, 0)
-        turn_vectors()
-        atten(0, 0, 0)
-        atten(0, 0, 1)
+        turn_flux()
+        attenuate(0, 0, 0)
+        attenuate(0, 0, 1)
         depth(0, 1, 1)
-        atten(0, 1, 0)
+        attenuate(0, 1, 0)
         cast_mu()
-        quant(-1, GF, GF + 1)
-        permute_mix(2)
+        quantise(1 - AHEAD, DTAU_SLOT, DTAU_SLOT + 1)
+        reorder_mix(2)
         depth(0, 2, 0)
-        atten(0, 1, 1)
+        attenuate(0, 1, 1)
         depth(0, 2, 1)
-        for k in range(NCH):
-            a, b = 2 * k - 3, 2 * k - 2
-            last = k == NCH - 1
-            times_rate(a)
-            store_y(a)
-            conv(b, 0)
-            conv(b, 1)
-            y_round(a - 1)
-            for c in X_END.get(k - 1, []):
-                x_exit(c)
+
+        for k in range(CHUNKS):
+            even = 2 * (k - 1)
+            odd = even + 1
+            before = even - 1
+            last = k == CHUNKS - 1
+            times_rate(before)
+            store_y(before)
+            conv(even, 0)
+            conv(even, 1)
+            y_round(before - 1)
+            if k - 1 in TURN_END:
+                dtau_exit(TURN_END[k - 1])
             if k == 1:
-                spread_exit(offset_bc, 32)
-            atten(k, 2, 0)
-            y_exit(a - 2)
+                nc.scalar.copy(out=offset_all[:].bitcast(F32), in_=offset_pairs)
+            attenuate(k, 2, 0)
+            y_exit(before - 2)
             if k == 1:
-                spread_exit(rate_bc, 64)
-            atten(k, 2, 1)
+                nc.scalar.copy(out=rate_all[:].bitcast(F32), in_=rate_pairs)
+            attenuate(k, 2, 1)
             if k == 0:
-                turn_columns()
+                turned = turn_vectors()
             if k < 2:
                 times_flux(k, 0, 1)
                 times_flux(k, 1, 2)
             else:
                 times_flux(k, 0, 2)
-            sunlit(b, 0)
+            sunlit(even, 0)
             if last:
-                y_quant(k - 3, 0, 1)
+                y_quantise(k - PLANES_LAG, 0, 1)
             else:
-                y_quant(k - 3)
-                store_codes(k - 3)
-            times_rate(b, 0, 1)
-            sunlit(b, 1)
-            times_rate(b, 1, 2)
-            if k == NCH - 2:
+                y_quantise(k - PLANES_LAG)
+                store_codes(k - PLANES_LAG)
+            times_rate(even, 0, 1)
+            sunlit(even, 1)
+            times_rate(even, 1, 2)
+            if k - PLANES_LAG == EARLY - 1:
                 store_early_scales()
-            store_y(b)
-            for c in X_MID.get(k, []):
-                x_turn(c)
+            store_y(even)
+            if k in TURN_MID:
+                dtau_turn(TURN_MID[k])
             depth(k + 1, 0, 0)
             depth(k + 1, 0, 1)
-            y_turn(a - 1)
-            atten(k + 1, 0, 0)
+            y_turn(before - 1)
+            attenuate(k + 1, 0, 0)
             if k == 0:
-                copy_columns()
-            for c in X_MID.get(k, []):
-                x_exit(c)
-            y_exit(a - 1)
-            y_round(a)
-            atten(k + 1, 0, 1)
-            conv(b + 1, 0)
-            conv(b + 1, 1)
+                copy_vectors(turned)
+            if k in TURN_MID:
+                dtau_exit(TURN_MID[k])
+            y_exit(before - 1)
+            y_round(before)
+            attenuate(k + 1, 0, 1)
+            conv(odd, 0)
+            conv(odd, 1)
             depth(k + 1, 1, 0)
             depth(k + 1, 1, 1)
-            y_turn(a)
+            y_turn(before)
             if k == 0:
-                spread(32)
-                spread(64)
-            for c in X_END.get(k, []):
-                x_turn(c)
-            atten(k + 1, 1, 0)
-            atten(k + 1, 1, 1)
+                offset_pairs = spread(OFFSET_ROW, "turn")
+                rate_pairs = spread(RATE_ROW, "turn")
+            if k in TURN_END:
+                dtau_turn(TURN_END[k])
+            attenuate(k + 1, 1, 0)
+            attenuate(k + 1, 1, 1)
             depth(k + 1, 2, 0)
             depth(k + 1, 2, 1)
             times_flux(k, 2, 3)
-            sunlit(b + 1, 0)
-            if k < NCH - 2:
-                sunlit(b + 1, 1)
-                quant(k, 0, GF + 1)
+            sunlit(odd, 0)
+            if k + AHEAD < CHUNKS:
+                sunlit(odd, 1)
+                quantise(k, 0, DTAU_SLOT + 1)
             elif not last:
-                quant(k, 0, 2)
-                sunlit(b + 1, 1)
-                quant(k, 2, 3)
-        y_exit(11)
-        quant(7, 0, 2)
-        quant(7, 2, 3)
-        y_quant(4, 1, 2)
-        store_codes(4)
-        y_quant(5)
-        store_codes(5)
-        sunlit(13, 1)
-        times_rate(13, 1, 2)
-        store_y(13, 1, 2)
-        times_rate(13, 0, 1)
-        store_y(13, 0, 1)
-        y_round(12)
-        conv(14, 0, "depth", 3)
-        conv(14, 1, "depth", 3)
-        conv(15, 0)
-        conv(15, 1)
-        y_turn(12)
-        sunlit(14, 0)
-        sunlit(14, 1)
-        sunlit(15, 0)
-        sunlit(15, 1)
-        y_round(13, 1, 2)
-        y_exit(12)
-        y_round(13, 0, 1)
-        y_turn(13)
-        times_rate(14, 0, 1, nc.vector)
-        store_y(14, 0, 1)
-        times_rate(14, 1, 2, nc.vector)
-        store_y(14, 1, 2)
-        y_round(14, 0, 1)
-        y_exit(13)
-        y_round(14, 1, 2)
-        times_rate(15, 0, 1, nc.vector)
-        store_y(15, 0, 1)
-        times_rate(15, 1, 2, nc.vector)
-        store_y(15, 1, 2)
-        y_round(15, 0, 1, True)
-        y_round(15, 1, 2, True)
-        y_quant(6)
-        store_codes(6)
-        y_turn(14)
-        y_turn(15, 1, 2, "depth", 3)
-        y_turn(15, 0, 1, "depth", 3)
-        y_exit(14)
-        y_exit(15, 1, 2, on_vector=True)
-        y_exit(15, 0, 1)
-        y_quant(7, 0, 2, 0, 1)
-        store_codes(7, 0, 2, 0, 1)
-        y_quant(7, 1, 2, 1, 2)
-        y_quant(7, 0, 1, 1, 2)
-        store_codes(7, 0, 2, 1, 2)
-        store_scales(M - LATE * CH, M, y_sc_last, [nc.scalar, nc.sync, nc.scalar, nc.sync])
+                quantise(k, 0, 2)
+                sunlit(odd, 1)
+                quantise(k, 2, 3)
+
+        final = CHUNKS - 1
+        even, odd = TILES - 2, TILES - 1
+        before = even - 1
+        pending = final - PLANES_LAG
+        rate_ps = spread(RATE_ROW, "depth").bitcast(BF16)
+        y_exit(before - 2)
+        sunlit(before, 1)
+        quantise(final, 0, 2)
+        quantise(final, 2, 3)
+        y_quantise(pending, 1, 2)
+        store_codes(pending)
+        y_quantise(pending + 1)
+        store_codes(pending + 1)
+        store_late_scales(pending, pending + 2, [nc.sync] * 4)
+        y_round(before - 1)
+        conv(even, 0, "depth")
+        conv(even, 1, "depth")
+        conv(odd, 0)
+        conv(odd, 1)
+        y_turn(before - 1)
+        times_rate(before, 0, 1, nc.vector, rate_ps)
+        store_y(before, 0, 1)
+        sunlit(even, 0)
+        times_rate(even, 0, 1)
+        times_rate(before, 1, 2, nc.vector, rate_ps)
+        store_y(before, 1, 2)
+        store_y(even, 0, 1)
+        sunlit(even, 1)
+        times_rate(even, 1, 2)
+        sunlit(odd, 0)
+        sunlit(odd, 1)
+        times_rate(odd, 0, 1, nc.vector, rate_ps)
+        store_y(even, 1, 2)
+        store_y(odd, 0, 1)
+        times_rate(odd, 1, 2, nc.vector, rate_ps)
+        store_y(odd, 1, 2)
+        y_round(before, 0, 1)
+        y_round(before, 1, 2)
+        y_turn(before)
+        y_round(even, 0, 1)
+        y_exit(before - 1)
+        y_exit(before)
+        y_round(even, 1, 2)
+        y_round(odd, 0, 1, nc.vector.tensor_copy)
+        y_round(odd, 1, 2, nc.vector.tensor_copy)
+        y_turn(even)
+        y_turn(odd, 0, 1, "conv")
+        y_turn(odd, 1, 2, "conv")
+        y_quantise(final - 1)
+        store_codes(final - 1)
+        y_exit(even)
+        y_exit(odd, 0, 1, nc.vector.tensor_copy)
+        y_exit(odd, 1, 2)
+        for j in range(2):
+            y_quantise(final, 0, LEVEL_GROUPS, j, j + 1)
+            store_codes(final, j, j + 1)
+        store_late_scales(pending + 2, CHUNKS, [nc.scalar, nc.sync, nc.scalar, nc.sync])

from contextlib import ExitStack

import concourse.mybir as mybir
from concourse.masks import make_identity

M, K, F, N = 2048, 512, 1536, 1024
FLOPS = 2 * M * K * F + 2 * M * F * N

F32 = mybir.dt.float32
BF16 = mybir.dt.bfloat16
I32 = mybir.dt.int32
U32 = mybir.dt.uint32
U8 = mybir.dt.uint8
FP8X4 = mybir.dt.float8_e4m3fn_x4
FP4X4 = mybir.dt.float4_e2m1fn_x4
ALU = mybir.AluOpType
ACT = mybir.ActivationFunctionType

P = 128
GROUP = 512
CHUNK = 256
CHUNKS = M // CHUNK
TILES = M // P
BAND_GROUPS = F // GROUP
LEVEL_GROUPS = N // GROUP
ALIGN = 256

BANKS = {"depth": 3, "conv": 2, "turn": 2}

AHEAD = 2
DTAU_SLOT = BAND_GROUPS
DTAU_LOADS = [(0, 1), (1, 2), (2, 4), (4, CHUNKS)]
TURN_MID = {0: 2, 1: 3}
TURN_END = {1: 4, 2: 5, 3: 6, 4: 7}
PLANES_LAG = 3
LATE = 4
EARLY = CHUNKS - LATE

OFFSET_ROW, RATE_ROW = 32, 64
PAIR_ROWS = N // (2 * P)


def tile_aerosol_albedo_heating_h1_kernel(
    tc, dtau, mix_words, mix_scales, flux, resp_words, resp_scales, mu0, offset, rate, out_0, out_1, out_2
):
    nc = tc.nc
    with ExitStack() as ctx:
        keep = ctx.enter_context(tc.tile_pool(name="keep", bufs=1))
        work = ctx.enter_context(tc.tile_pool(name="work", bufs=1))
        psum = ctx.enter_context(tc.psum_pool(name="psum", bufs=1))
        ctx.enter_context(tc.manual_schedule())

        def bank(role, shape):
            return psum.tile(shape, F32, name=role, tag=role, bufs=BANKS[role])

        def levels(s0, s1):
            return slice(GROUP * s0, GROUP * s1)

        ident = keep.tile([P, P], F32, name="ident")
        flux_raw = keep.tile([P, GROUP], BF16, name="flux_raw")
        mu_raw = keep.tile([P, P], BF16, name="mu_raw")
        vec_rows = keep.tile([P, P], F32, name="vec_rows")
        vec_cols = keep.tile([P, RATE_ROW + PAIR_ROWS], F32, name="vec_cols")
        flux_rows = keep.tile([P, 4, P], F32, name="flux_rows")
        mix_sc_raw = keep.tile([P, F], U8, name="mix_sc_raw", align_bytes=ALIGN)
        mix_w_first = keep.tile([P, 2 * GROUP], U8, name="mix_w_first", align_bytes=ALIGN)
        mix_w_rest = keep.tile([P, 2 * (F - GROUP)], U8, name="mix_w_rest", align_bytes=ALIGN)
        mix_w = keep.tile([P, BAND_GROUPS, 4, 2 * P], U8, name="mix_w", align_bytes=ALIGN)
        mix_sc = keep.tile([P, BAND_GROUPS, 4, P], U8, name="mix_sc", align_bytes=ALIGN)
        resp_w = keep.tile([P, BAND_GROUPS, 2 * N], U8, name="resp_w", align_bytes=ALIGN)
        resp_sc = keep.tile([P, BAND_GROUPS, N], U8, name="resp_sc", align_bytes=ALIGN)
        offset_all = keep.tile([P, N], BF16, name="offset_all")
        rate_all = keep.tile([P, N], BF16, name="rate_all")
        y_sc_early = keep.tile([P, EARLY, LEVEL_GROUPS, CHUNK], U8, name="y_sc_early", align_bytes=ALIGN)
        y_sc_late = keep.tile([P, LEVEL_GROUPS, LATE * CHUNK], U8, name="y_sc_late", align_bytes=ALIGN)
        flux_ps = psum.tile([P, P, 4], F32, name="flux_ps")

        dtau_sb = {}

        def load_dtau(c0, c1):
            rows = keep.tile([P, 2 * (c1 - c0), K], BF16, name="dtau%d" % c0, align_bytes=ALIGN)
            nc.sync.dma_start(out=rows[:], in_=dtau[CHUNK * c0 : CHUNK * c1, :].rearrange("(j p) k -> p j k", p=P))
            for c in range(c0, c1):
                dtau_sb[c] = rows[:, 2 * (c - c0) : 2 * (c - c0) + 2, :]

        nc.vector.memset(mix_sc_raw[:].bitcast(I32), 0)
        nc.vector.memset(resp_sc[:].rearrange("p g n -> p (g n)").bitcast(I32), 0)
        nc.gpsimd.dma_start(out=flux_raw[0:BAND_GROUPS, :], in_=flux.rearrange("(g k) -> g k", g=BAND_GROUPS))
        make_identity(nc, ident[:])
        nc.scalar.activation(out=vec_rows[:], in_=ident[:], func=ACT.Copy, scale=0.0)
        nc.gpsimd.memset(flux_rows[:], 0.0)

        load_dtau(*DTAU_LOADS[0])
        nc.sync.dma_start(out=mix_w_first[:].bitcast(I32), in_=mix_words[0, :, 0 : 2 * GROUP].bitcast(I32))
        for q in range(4):
            nc.sync.dma_start(
                out=mix_sc_raw[32 * q : 32 * q + 4, :].bitcast(I32), in_=mix_scales[0, 4 * q : 4 * q + 4, :].bitcast(I32)
            )
        load_dtau(*DTAU_LOADS[1])
        nc.sync.dma_start(out=mix_w_rest[:].bitcast(I32), in_=mix_words[0, :, 2 * GROUP : 2 * F].bitcast(I32))
        load_dtau(*DTAU_LOADS[2])
        nc.sync.dma_start(out=mu_raw[0:TILES, :], in_=mu0.rearrange("(i p) -> i p", p=P))
        for vec, row in ((offset, OFFSET_ROW), (rate, RATE_ROW)):
            nc.sync.dma_start(
                out=vec_rows[row : row + PAIR_ROWS, :].bitcast(I32),
                in_=vec.rearrange("(j w) -> j w", j=PAIR_ROWS).bitcast(I32),
            )
        nc.sync.dma_start(out=resp_w[:].bitcast(I32), in_=resp_words.rearrange("g p b -> p g b").bitcast(I32))
        for q in range(4):
            nc.sync.dma_start(
                out=resp_sc[32 * q : 32 * q + 4, :, :].bitcast(I32),
                in_=resp_scales[:, 4 * q : 4 * q + 4, :].rearrange("g r n -> r g n").bitcast(I32),
            )
        load_dtau(*DTAU_LOADS[3])

        def reorder_mix(g):
            words = mix_w_first[:] if g == 0 else mix_w_rest[:, 2 * GROUP * (g - 1) : 2 * GROUP * g]
            nc.vector.tensor_copy(
                out=mix_w[:, g, :, :].rearrange("p t (m b) -> p t m b", b=2),
                in_=words.rearrange("p (m t b) -> p t m b", t=4, b=2),
            )
            nc.vector.tensor_copy(
                out=mix_sc[:, g, :, :],
                in_=mix_sc_raw[:, GROUP * g : GROUP * (g + 1)].rearrange("p (m t) -> p t m", t=4),
            )

        def cast_flux():
            nc.scalar.copy(
                out=flux_rows[0:BAND_GROUPS, :, :], in_=flux_raw[0:BAND_GROUPS, :].rearrange("g (p t) -> g t p", t=4)
            )

        def turn_flux():
            for t in range(4):
                nc.tensor.transpose(flux_ps[:, :, t], flux_rows[:, t, :], ident[:])

        def cast_mu():
            nc.scalar.copy(out=vec_rows[0:TILES, :], in_=mu_raw[0:TILES, :])

        def turn_vectors():
            turned = bank("conv", [P, P])
            nc.tensor.transpose(turned[:], vec_rows[:], ident[:])
            return turned

        def copy_vectors(turned):
            nc.scalar.copy(out=vec_cols[:], in_=turned[:, 0 : RATE_ROW + PAIR_ROWS])

        def spread(row, role):
            pairs = bank(role, [P, PAIR_ROWS, P])
            for j in range(PAIR_ROWS):
                nc.tensor.transpose(pairs[:, j, :], vec_cols[:, row + j : row + j + 1].to_broadcast([P, P]), ident[:])
            return pairs[:].rearrange("p j w -> p (j w)")

        dtau_ps, depth_ps, decay, unquantised, codes, scales = {}, {}, {}, {}, {}, {}

        def slots(c):
            if c not in unquantised:
                unquantised[c] = work.tile(
                    [P, BAND_GROUPS + 1, CHUNK * 4], BF16, name="unquantised", tag="unquantised", bufs=5, align_bytes=ALIGN
                )
            return unquantised[c]

        def dtau_turn(c):
            dtau_ps[c] = bank("turn", [P, 2, 2, P])
            for j in range(2):
                pairs = dtau_sb[c][:, j, :].bitcast(F32)
                for u in range(2):
                    nc.tensor.transpose(dtau_ps[c][:, j, u, :], pairs[:, u : K // 2 : 2], ident[:])

        def dtau_exit(c):
            nc.scalar.copy(
                out=slots(c - AHEAD)[:, DTAU_SLOT, :].bitcast(F32).rearrange("p (j r u) -> p j r u", j=2, u=2),
                in_=dtau_ps[c][:].rearrange("p j u r -> p j r u"),
            )

        def quantise(c, slot0, slot1):
            if c not in codes:
                width = (BAND_GROUPS + 1) * CHUNK
                codes[c] = work.tile([P, width], U32, name="codes", tag="codes", bufs=4, align_bytes=ALIGN)
                scales[c] = work.tile([P, width], U8, name="scales", tag="scales", bufs=4, align_bytes=ALIGN)
            nc.vector.quantize_mx(
                out=codes[c][:, CHUNK * slot0 : CHUNK * slot1].bitcast(FP8X4),
                scales=scales[c][:, CHUNK * slot0 : CHUNK * slot1],
                in_=unquantised[c][:, slot0:slot1, :].rearrange("p g x -> p (g x)"),
            )

        def depth(c, g, u):
            if c >= CHUNKS:
                return
            depth_ps[c, g, u] = bank("depth", [P, 2, CHUNK])
            for e in range(2):
                nc.tensor.matmul_mx(
                    out=depth_ps[c, g, u][:, e, :],
                    lhsT=mix_w[:, g, 2 * u + e, :].bitcast(FP4X4),
                    lhsT_scale=mix_sc[:, g, 2 * u + e, :],
                    rhs=codes[c - AHEAD][:, DTAU_SLOT * CHUNK :].bitcast(FP8X4),
                    rhs_scale=scales[c - AHEAD][:, DTAU_SLOT * CHUNK :],
                    start=True,
                    stop=True,
                )

        def attenuate(c, g, u):
            if c >= CHUNKS:
                return
            if c not in decay:
                decay[c] = work.tile([P, 2, BAND_GROUPS, CHUNK, 2], F32, name="decay", tag="decay", bufs=2)
            nc.scalar.activation(
                out=decay[c][:, u, g, :, :],
                in_=depth_ps[c, g, u][:].rearrange("p e m -> p m e"),
                func=ACT.Exp,
                scale=-1.0,
            )

        def times_flux(c, g0, g1):
            shape = [P, g1 - g0, CHUNK, 2, 2]
            nc.vector.tensor_tensor(
                out=slots(c)[:, g0:g1, :].rearrange("p g (m u e) -> p g m u e", u=2, e=2),
                in0=decay[c][:, :, g0:g1, :, :].rearrange("p u g m e -> p g m u e"),
                in1=flux_ps[:, g0:g1, :].rearrange("p g (u e) -> p g u e", u=2).unsqueeze(2).to_broadcast(shape),
                op=ALU.mult,
            )

        conv_ps, sunlit_sb, y, y_pairs, y_ps, y_turned, y_codes = {}, {}, {}, {}, {}, {}, {}

        def conv(i, s, role="conv"):
            if i < 0:
                return
            c, j = divmod(i, 2)
            conv_ps[i, s] = bank(role, [P, GROUP])
            for g in range(BAND_GROUPS):
                scenes = slice(CHUNK * g + P * j, CHUNK * g + P * (j + 1))
                nc.tensor.matmul_mx(
                    out=conv_ps[i, s][:],
                    lhsT=codes[c][:, scenes].bitcast(FP8X4),
                    lhsT_scale=scales[c][:, scenes],
                    rhs=resp_w[:, g, 2 * GROUP * s : 2 * GROUP * (s + 1)].bitcast(FP4X4),
                    rhs_scale=resp_sc[:, g, levels(s, s + 1)],
                    start=(g == 0),
                    stop=(g == BAND_GROUPS - 1),
                )

        def sunlit(i, s):
            if i < 0:
                return
            if i not in sunlit_sb:
                sunlit_sb[i] = work.tile([P, N], F32, name="sunlit", tag="sunlit", bufs=3)
            nc.vector.scalar_tensor_tensor(
                out=sunlit_sb[i][:, levels(s, s + 1)],
                in0=conv_ps[i, s][:],
                scalar=vec_cols[:, i : i + 1],
                in1=offset_all[:, levels(s, s + 1)],
                op0=ALU.mult,
                op1=ALU.add,
            )

        def times_rate(i, s0=0, s1=LEVEL_GROUPS, engine=nc.gpsimd, factor=rate_all):
            if i < 0:
                return
            if i not in y:
                y[i] = work.tile([P, N], F32, name="y", tag="y", bufs=4, align_bytes=ALIGN)
            cols = levels(s0, s1)
            engine.tensor_tensor(out=y[i][:, cols], in0=sunlit_sb[i][:, cols], in1=factor[:, cols], op=ALU.mult)

        def store_y(i, s0=0, s1=LEVEL_GROUPS):
            if i < 0:
                return
            nc.sync.dma_start(out=out_0[P * i : P * (i + 1), levels(s0, s1)], in_=y[i][:, levels(s0, s1)])

        def y_round(i, s0=0, s1=LEVEL_GROUPS, copy=nc.scalar.copy):
            if i < 0:
                return
            if i not in y_pairs:
                y_pairs[i] = work.tile([P, 2, LEVEL_GROUPS, P, 2], BF16, name="y_pairs", tag="y_pairs", bufs=4)
            copy(
                out=y_pairs[i][:, :, s0:s1, :, :],
                in_=y[i][:, levels(s0, s1)].rearrange("p (s q u e) -> p u s q e", q=P, u=2, e=2),
            )

        def y_turn(i, s0=0, s1=LEVEL_GROUPS, role="turn"):
            if i < 0:
                return
            y_ps[i, s0] = bank(role, [P, s1 - s0, 2, P])
            for s in range(s0, s1):
                for u in range(2):
                    pairs = y_pairs[i][:, u, s, :, :].rearrange("p q e -> p (q e)").bitcast(F32)
                    nc.tensor.transpose(y_ps[i, s0][:, s - s0, u, :], pairs, ident[:])

        def y_exit(i, s0=0, s1=LEVEL_GROUPS, copy=nc.scalar.copy):
            if i < 0:
                return
            c, j = divmod(i, 2)
            if c not in y_turned:
                y_turned[c] = work.tile(
                    [P, LEVEL_GROUPS, CHUNK * 4], BF16, name="y_turned", tag="y_turned", bufs=3, align_bytes=ALIGN
                )
            copy(
                out=y_turned[c][:, s0:s1, 4 * P * j : 4 * P * (j + 1)].bitcast(F32).rearrange("p s (r u) -> p s r u", u=2),
                in_=y_ps[i, s0][:].rearrange("p s u r -> p s r u"),
            )

        def y_quantise(c, s0=0, s1=LEVEL_GROUPS, j0=0, j1=2):
            if c < 0:
                return
            if c not in y_codes:
                y_codes[c] = work.tile(
                    [P, LEVEL_GROUPS, CHUNK], U32, name="y_codes", tag="y_codes", bufs=CHUNKS, align_bytes=ALIGN
                )
            if c < EARLY:
                nc.vector.quantize_mx(
                    out=y_codes[c][:].rearrange("p s m -> p (s m)").bitcast(FP8X4),
                    scales=y_sc_early[:, c, :, :].rearrange("p s m -> p (s m)"),
                    in_=y_turned[c][:].rearrange("p s x -> p (s x)"),
                )
                return
            m0 = CHUNK * (c - EARLY)
            for s in range(s0, s1):
                nc.vector.quantize_mx(
                    out=y_codes[c][:, s, P * j0 : P * j1].bitcast(FP8X4),
                    scales=y_sc_late[:, s, m0 + P * j0 : m0 + P * j1],
                    in_=y_turned[c][:, s, 4 * P * j0 : 4 * P * j1],
                )

        def store_codes(c, j0=0, j1=2):
            if c < 0:
                return
            scenes = slice(CHUNK * c + P * j0, CHUNK * c + P * j1)
            nc.sync.dma_start(
                out=out_1[:, :, scenes, :].rearrange("g p m t -> p g (m t)").bitcast(I32),
                in_=y_codes[c][:, :, P * j0 : P * j1].bitcast(I32),
            )

        def store_early_scales():
            for s in range(LEVEL_GROUPS):
                for q in range(4):
                    nc.sync.dma_start(
                        out=out_2[s, 4 * q : 4 * q + 4, 0 : EARLY * CHUNK].rearrange("r (c m) -> r c m", m=CHUNK).bitcast(I32),
                        in_=y_sc_early[32 * q : 32 * q + 4, :, s, :].bitcast(I32),
                    )

        def store_late_scales(c0, c1, queues):
            for q in range(4):
                queues[q].dma_start(
                    out=out_2[:, 4 * q : 4 * q + 4, CHUNK * c0 : CHUNK * c1].rearrange("g r m -> r g m").bitcast(I32),
                    in_=y_sc_late[32 * q : 32 * q + 4, :, CHUNK * (c0 - EARLY) : CHUNK * (c1 - EARLY)].bitcast(I32),
                )

        dtau_turn(0)
        dtau_exit(0)
        dtau_turn(1)
        reorder_mix(0)
        quantise(0 - AHEAD, DTAU_SLOT, DTAU_SLOT + 1)
        dtau_exit(1)
        cast_flux()
        depth(0, 0, 0)
        depth(0, 0, 1)
        reorder_mix(1)
        depth(0, 1, 0)
        turn_flux()
        attenuate(0, 0, 0)
        attenuate(0, 0, 1)
        depth(0, 1, 1)
        attenuate(0, 1, 0)
        cast_mu()
        quantise(1 - AHEAD, DTAU_SLOT, DTAU_SLOT + 1)
        reorder_mix(2)
        depth(0, 2, 0)
        attenuate(0, 1, 1)
        depth(0, 2, 1)

        for k in range(CHUNKS):
            even = 2 * (k - 1)
            odd = even + 1
            before = even - 1
            last = k == CHUNKS - 1
            times_rate(before)
            store_y(before)
            conv(even, 0)
            conv(even, 1)
            y_round(before - 1)
            if k - 1 in TURN_END:
                dtau_exit(TURN_END[k - 1])
            if k == 1:
                nc.scalar.copy(out=offset_all[:].bitcast(F32), in_=offset_pairs)
            attenuate(k, 2, 0)
            y_exit(before - 2)
            if k == 1:
                nc.scalar.copy(out=rate_all[:].bitcast(F32), in_=rate_pairs)
            attenuate(k, 2, 1)
            if k == 0:
                turned = turn_vectors()
            if k < 2:
                times_flux(k, 0, 1)
                times_flux(k, 1, 2)
            else:
                times_flux(k, 0, 2)
            sunlit(even, 0)
            if last:
                y_quantise(k - PLANES_LAG, 0, 1)
            else:
                y_quantise(k - PLANES_LAG)
                store_codes(k - PLANES_LAG)
            times_rate(even, 0, 1)
            sunlit(even, 1)
            times_rate(even, 1, 2)
            if k - PLANES_LAG == EARLY - 1:
                store_early_scales()
            store_y(even)
            if k in TURN_MID:
                dtau_turn(TURN_MID[k])
            depth(k + 1, 0, 0)
            depth(k + 1, 0, 1)
            y_turn(before - 1)
            attenuate(k + 1, 0, 0)
            if k == 0:
                copy_vectors(turned)
            if k in TURN_MID:
                dtau_exit(TURN_MID[k])
            y_exit(before - 1)
            y_round(before)
            attenuate(k + 1, 0, 1)
            conv(odd, 0)
            conv(odd, 1)
            depth(k + 1, 1, 0)
            depth(k + 1, 1, 1)
            y_turn(before)
            if k == 0:
                offset_pairs = spread(OFFSET_ROW, "turn")
                rate_pairs = spread(RATE_ROW, "turn")
            if k in TURN_END:
                dtau_turn(TURN_END[k])
            attenuate(k + 1, 1, 0)
            attenuate(k + 1, 1, 1)
            depth(k + 1, 2, 0)
            depth(k + 1, 2, 1)
            times_flux(k, 2, 3)
            sunlit(odd, 0)
            if k + AHEAD < CHUNKS:
                sunlit(odd, 1)
                quantise(k, 0, DTAU_SLOT + 1)
            elif not last:
                quantise(k, 0, 2)
                sunlit(odd, 1)
                quantise(k, 2, 3)

        final = CHUNKS - 1
        even, odd = TILES - 2, TILES - 1
        before = even - 1
        pending = final - PLANES_LAG
        rate_ps = spread(RATE_ROW, "depth").bitcast(BF16)
        y_exit(before - 2)
        sunlit(before, 1)
        quantise(final, 0, 2)
        quantise(final, 2, 3)
        y_quantise(pending, 1, 2)
        store_codes(pending)
        y_quantise(pending + 1)
        store_codes(pending + 1)
        store_late_scales(pending, pending + 2, [nc.sync] * 4)
        y_round(before - 1)
        conv(even, 0, "depth")
        conv(even, 1, "depth")
        conv(odd, 0)
        conv(odd, 1)
        y_turn(before - 1)
        times_rate(before, 0, 1, nc.vector, rate_ps)
        store_y(before, 0, 1)
        sunlit(even, 0)
        times_rate(even, 0, 1)
        times_rate(before, 1, 2, nc.vector, rate_ps)
        store_y(before, 1, 2)
        store_y(even, 0, 1)
        sunlit(even, 1)
        times_rate(even, 1, 2)
        sunlit(odd, 0)
        sunlit(odd, 1)
        times_rate(odd, 0, 1, nc.vector, rate_ps)
        store_y(even, 1, 2)
        store_y(odd, 0, 1)
        times_rate(odd, 1, 2, nc.vector, rate_ps)
        store_y(odd, 1, 2)
        y_round(before, 0, 1)
        y_round(before, 1, 2)
        y_turn(before)
        y_round(even, 0, 1)
        y_exit(before - 1)
        y_exit(before)
        y_round(even, 1, 2)
        y_round(odd, 0, 1, nc.vector.tensor_copy)
        y_round(odd, 1, 2, nc.vector.tensor_copy)
        y_turn(even)
        y_turn(odd, 0, 1, "conv")
        y_turn(odd, 1, 2, "conv")
        y_quantise(final - 1)
        store_codes(final - 1)
        y_exit(even)
        y_exit(odd, 0, 1, nc.vector.tensor_copy)
        y_exit(odd, 1, 2)
        for j in range(2):
            y_quantise(final, 0, LEVEL_GROUPS, j, j + 1)
            store_codes(final, j, j + 1)
        store_late_scales(pending + 2, CHUNKS, [nc.scalar, nc.sync, nc.scalar, nc.sync])
